import numpy as np, ml_dtypes
CORES = [48,51,52,55]
N = 4
import mx_ref
BF = ml_dtypes.bfloat16
def tile(rs):
    return np.stack(rs, axis=2).reshape(128, -1).astype(BF)
def pick(q, e):
    c = np.concatenate([q[0].reshape(128, -1, 4), np.zeros((128, 1, 4), np.uint8)], axis=1); s = np.concatenate([q[1], np.ones((16, 1), np.uint8)], axis=1)
    return (np.ascontiguousarray(c[:, e].reshape(128, -1)), np.ascontiguousarray(s[:, e]))
def join(*qs):
    return (np.concatenate([q[0] for q in qs], axis=1), np.concatenate([q[1] for q in qs], axis=1))
def put(q, e, v):
    c, s = q[0].reshape(128, -1, 4).copy(), q[1].copy(); c[:, e] = v[0].reshape(128, -1, 4); s[:, e] = v[1]
    return (c.reshape(128, -1), s)
def pk(c, s):
    return (np.ascontiguousarray(c), mx_ref.live(s))
def emit(q):
    return q[0], q[1]
def packed(v, rng):
    q = [mx_ref.quantize(np.ascontiguousarray(v[r])) for r in range(N)]
    return np.stack([a for a, b in q]), np.stack([mx_ref.plane(b, rng) for a, b in q])
def values_of_codes():
    e, c = np.zeros((128, 128, 4), np.float32), np.zeros((128, 2, 4), np.uint8)
    e[np.arange(128), np.arange(128), 0] = 1
    c[:127, :, 0] = np.arange(256).reshape(2, 128).T[:127]
    return mx_ref.matmul(mx_ref.quantize(e.reshape(128, 512).astype(BF)), (c.reshape(128, 8), np.full((16, 2), 127, np.uint8))).T.reshape(-1).astype(np.float64)
CODE_VALUE, SCALE_VALUE = values_of_codes(), 2.0 ** (np.arange(256) - 127.0)
def decode(q):
    return (CODE_VALUE[q[0]].reshape(16, 8, -1, 4) * SCALE_VALUE[q[1]][:, None, :, None] + 0.0).reshape(128, -1).astype(np.float32)
def f(rng, *shape):
    return mx_ref.flush((rng.standard_normal(shape, dtype=np.float32) * np.exp2(rng.integers(-2, 3, shape[:-1] + (1,)))).astype(BF))
def wide(rng, *shape, cols=0):
    v = rng.standard_normal(shape, dtype=np.float32) * np.exp2(rng.integers(-12, 13, shape)).astype(np.float32)
    if cols: v *= np.repeat(np.exp2(rng.integers(-cols, cols + 1, shape[:-2] + (1, shape[-1] // 4))) * (rng.random(shape[:-2] + (1, shape[-1] // 4)) > 0.0625), 4, axis=-1).astype(np.float32)
    return mx_ref.flush(v.astype(BF))
C, H = 320, 160
MASK = [1, 2, 3]
def numbers_of(rng):
    return {"x": np.array(f(rng, N, 128, 4 * C)), "u": np.array(f(rng, N, 128, 512)), "v": np.array(f(rng, N, 128, 512))}
def weights(rng, w):
    c, s = packed(np.ascontiguousarray(w).reshape(N, 128, 2048), rng)
    return {"wc": c, "ws": s}
def layers(rng, still=[], pairs=False):
    w = np.array(f(rng, N, 128, 2048)).reshape(N, 8, 16, 4, 8, 16, 4)
    for i in still:
        w[:, :, i] = 0
        w[:, :, :, :, :, i] = 0
    if pairs:
        w[:, :, :, :, :, 8:] = 0
        for g in range(8):
            w[:, g, 8, 0, g, 8, 0] = -28.0
            for b in range(4): w[:, g, 10, b, g, 9, 0] = -2.0 ** (b - 5)
    return weights(rng, w)
def setup_inputs(rng):
    return {**numbers_of(rng), **layers(rng)}
def setup_inputs_ties(rng):
    d = numbers_of(rng)
    o = rng.permutation(N)
    k = rng.integers(0, 4, (N, 8, C))
    k[o[1]] += 1
    k[o[2], rng.permutation(8)[:4]] = 1
    for g in range(8): k[o[3], g] = 1 + (rng.permutation(C) < H + g % 3 - 1)
    x = d["x"].reshape(N, 8, 16, C, 4)
    x[:, :, 0] = 0
    x[:, :, 0, :, 0] = k.astype(np.float32).astype(BF)
    a = np.exp2(rng.integers(-3, 4, (N, 8, C)).astype(np.float32))
    x[:, :, 8:] = 0
    x[:, :, 8, :, 0] = (-1.125 * a).astype(BF)
    x[:, :, 10, :, 0] = (-0.0703125 * a).astype(BF)
    u = d["u"].reshape(N, 128, 128, 4)
    u[:, :, ::16] = 0
    for r in range(N):
        for h in range(0, 128, 16): u[r, h, h, 0] = 0.0 if r == o[0] else -1.0 if r == o[1] else 1.0
    return {"x": x.reshape(N, 128, 4 * C), "u": u.reshape(N, 128, 512), "v": d["v"], **layers(rng, [0], True)}
def setup_inputs_near(rng):
    d = numbers_of(rng)
    x = d["x"].astype(np.float32).reshape(N, 8, 16, C, 4)
    x[:, :, 0] = 0
    x[:, :, 8:] = 0
    u = d["u"].reshape(N, 128, 128, 4)
    u[:, :, ::16] = 0
    o = rng.permutation(N) % 4
    for r in range(N):
        c = rng.choice([-1.0, 1.0], (8, 1))
        s = rng.integers(0, 16, (8, C))
        digits = ((s[:, :, None] >> np.arange(4)) & 1) * np.exp2(np.arange(4) - 23.0)
        if o[r] < 2:
            x[r, :, 0, :, 0] = c
            x[r, :, 8] = digits
            x[r, :, 11, :, 0] = 2.0 ** -10
        elif o[r] == 2: x[r, :, 8] = digits * rng.choice([-1.0, 1.0], (8, C, 1))
        else:
            x[r, :, 8, :, 0] = np.where(s < 8, 1.25, 0.0) * 2.0 ** -30 * c
            x[r, :, 9, :, 0] = np.where(s < 8, 0.0, 1.125) * 2.0 ** -30 * c
            for g in rng.permutation(8)[:4]:
                e = rng.choice([-1.0, 1.0], C) * 2.0 ** -30
                x[r, g, 8, :, 0] = 1.25 * e
                x[r, g, 9, :, 0] = -1.125 * e
        at = [0, C - 1, int(rng.integers(C)), int(rng.integers(C))]
        for g, j in zip(rng.permutation(8)[:4], at): x[r, g, 0, j, 0] = 2.0 ** 29 * rng.choice([-1.0, 1.0])
        k = 1.0 if o[r] == 0 else 2.0 ** -30
        for h in range(0, 128, 16):
            u[r, h, h, 0] = k if o[r] < 2 else 1.0
            if o[r] < 2: u[r, h + 11, h, 0] = k
            if o[r] < 3: u[r, h + 8, h] = k
            else:
                u[r, h + 8, h, 0] = k
                u[r, h + 9, h, 0] = 1.125 * k
    return {"x": x.reshape(N, 128, 4 * C).astype(BF), "u": u.reshape(N, 128, 512), "v": d["v"], **layers(rng, [0, 8, 9, 10, 11, 12, 13, 14, 15])}
def setup_inputs_odd(rng):
    d = numbers_of(rng)
    o = rng.permutation(N)
    x = (1.0 + (2 * rng.integers(0, 64, (N, 16, 8, C, 4)) + 1) * 2.0 ** -7) * np.exp2(-rng.integers(0, 7, (N, 16, 8, C, 4)).astype(np.float64)) * rng.choice([-1.0, 1.0], (N, 16, 8, C, 4))
    s = rng.choice([-1.0, 1.0], (N, 8, 2, C))
    late = np.arange(C) >= H
    e = np.arange(C)[None, :] - np.where(np.arange(8)[:, None] < rng.integers(1, 8), 1, 0)
    s[o[0], :, 0] = np.where(late, 1.0, -1.0)
    s[o[1], :, 0] = np.where((e >= 0) & (e < H), 1.0, -1.0)
    s[o[2], :, 0] = np.where(late[None, :] == (rng.permutation(8)[:, None] < 4), 1.0, -1.0)
    x[:, :, 0, :, 0] = 1.96875 * 2.0 ** 8 * s.reshape(N, 16, C)
    u = d["u"].reshape(N, 16, 8, 128, 4)
    u[:, :, 0, ::16] = 0
    for r in o[:3]:
        u[r, :, :, ::16] = 0
        for g in range(8): u[r, 2 * g, 0, 16 * g, 0] = 1.0
    for i, g in enumerate(rng.permutation(8)[:4]):
        x[o[3], 2 * g, 1, :, 0] = (8 + rng.integers(0, 2, C)) * 2.0 ** (i - 8)
        u[o[3], :, :, 16 * g] = 0
        u[o[3], 2 * g, 1, 16 * g, 0] = 1.0
    return {"x": x.astype(np.float32).reshape(N, 128, 4 * C).astype(BF), "u": u.reshape(N, 128, 512), "v": d["v"], **layers(rng, [0, 8])}
def setup_inputs_ends(rng):
    d = numbers_of(rng)
    x = np.zeros((N, 8, 16, C, 4))
    u = d["u"].astype(np.float32).reshape(N, 128, 128, 4)
    v = d["v"].astype(np.float32)
    w = np.zeros((N, 128, 4, 128, 4), np.float32)
    o = rng.permutation(N) % 4
    i = np.arange(128)
    for r in range(N):
        h = rng.permutation(8)
        c = np.where(h < 2, 0.0, h % 2 * 2.0 - 1.0)[None, :, None]
        low = -(0.9 + 0.1 * rng.random((8, 16, C, 4))) * 2.0 ** 30
        if o[r] == 0: x[r] = low
        if o[r] == 1: x[r] = np.where((rng.random(C) < 0.5)[:, None], (1.0 + 0.4 * rng.random((8, 16, C, 4))) * 2.0 ** 27, low)
        if o[r] == 2: x[r] = -(1.0 + 0.125 * rng.integers(0, 8, (8, 16, C, 4))) * 2.0 ** -30
        if o[r] == 3: x[r] = d["x"][r].astype(np.float32).reshape(8, 16, C, 4)[:, :, :1]
        if o[r] < 2:
            u[r, :, ::16] = c * (0.9 + 0.1 * rng.random((128, 8, 4))) * 2.0 ** 30
            v[r] = rng.choice([-1.0, 1.0], (128, 512)) * (0.9 + 0.1 * rng.random((128, 512))) * 2.0 ** 30
        if o[r] == 2:
            u[r, :, ::16] = c * (1.0 + 0.125 * rng.integers(0, 8, (128, 8, 4))) * 2.0 ** -30
            v[r] = rng.choice([-1.0, 1.0], (128, 512)) * (1.0 + 0.125 * rng.integers(0, 8, (128, 512))) * 2.0 ** -30
        if o[r] == 3: u[r, :, ::16] *= np.abs(c).astype(np.float32)
        k = np.array([4.0, 8.0, 16.0])[rng.permutation(8) % 3]
        for b in range(4): w[r, i, b, i, b] = k[i // 16]
    return {"x": x.astype(np.float32).reshape(N, 128, 4 * C).astype(BF), "u": u.reshape(N, 128, 512).astype(BF), "v": v.astype(BF), **weights(rng, w.astype(BF))}
def setup_inputs_spread(rng):
    d = setup_inputs(rng)
    d["x"] = wide(rng, N, 128, 4 * C, cols=6)
    return d
def check_inputs(d):
    b = []
    for k in ("x", "u", "v"):
        a = np.abs(d[k].astype(np.float32))
        if not (np.isfinite(a).all() and ((a == 0) | (a >= 2.0 ** -30) & (a <= 2.0 ** 30)).all()): b.append("a value of " + k)
    none, least, most = [emit(mx_ref.quantize(np.full((128, 16), k, np.float32).astype(BF)))[1][0, 0] for k in (0.0, 2.0 ** -8, 2.0 ** 8)]
    for r in range(N):
        if ((d["wc"][r] == 0x7F) | (d["wc"][r] == 0xFF)).any(): b.append("wc: a code that is no number")
        s = mx_ref.live(d["ws"][r])
        if ((s != none) & ((s < least) | (s > most))).any(): b.append("ws: a scale out of range")
    return b
def parts(t):
    return np.ascontiguousarray(t.reshape(8, 16, -1, 4).transpose(2, 0, 1, 3)).reshape(-1, 16, 4)
def laid(p):
    return np.ascontiguousarray(p.reshape(-1, 8, 16, 4).transpose(1, 2, 0, 3)).reshape(128, -1)
def layer(w, q):
    return mx_ref.quantize(tile([np.maximum(mx_ref.matmul(pick(w, np.arange(128 * b, 128 * b + 128)), q), np.float32(0.0)) * np.float32(0.03125) for b in range(4)]))
def reference(x, u, v, wc, ws):
    qu = [mx_ref.quantize(u[r]) for r in range(N)]
    lay = [pk(wc[r], ws[r]) for r in range(N)]
    now = [x[r] for r in range(N)]
    for m in MASK:
        t, high, low, own, out = [], [], [], [], []
        for r in range(N):
            q = mx_ref.quantize(now[r])
            s = mx_ref.matmul(qu[r], q)[::16] + np.float32(0.0)
            flag = np.zeros((8, C), bool)
            np.put_along_axis(flag, np.argsort(-s, axis=1, kind="stable")[:, :H], True, axis=1)
            high.append(np.flatnonzero(flag.T))
            low.append(np.flatnonzero(~flag.T))
            t.append(decode(q))
            p = parts(t[r].astype(BF))
            own.append(mx_ref.quantize(laid(p[high[r]])))
            out.append(mx_ref.quantize(laid(p[low[r]])))
        home = [layer(lay[r], own[r]) for r in range(N)]
        guest = [layer(lay[r], out[r ^ m]) for r in range(N)]
        for r in range(N):
            a = np.zeros((8 * C, 16, 4), np.float32)
            a[high[r]] = parts(decode(home[r]))
            a[low[r]] = parts(decode(guest[r ^ m]))
            now[r] = (t[r] + laid(a)).astype(BF)
    y, op = np.zeros((N, 128, C), np.float32), np.zeros((N, 8, C), np.float32)
    oc, osc = np.zeros((N, 128, 4 * C), np.uint8), np.zeros((N, 16, C), np.uint8)
    for r in range(N):
        q = mx_ref.quantize(now[r])
        y[r] = mx_ref.matmul(mx_ref.quantize(v[r]), q)
        n = np.zeros(8 * C, np.int64)
        n[high[r]] = np.arange(4 * C)
        n[low[r]] = 4 * C + np.arange(4 * C)
        op[r] = n.reshape(C, 8).T
        oc[r], osc[r] = emit(q)
    return {"y": y, "op": op, "oc": oc, "osc": osc}

@@ -1,0 +1,535 @@
+import math
+from concourse.mybir import dt, AluOpType as Op, ActivationFunctionType as Fn
+
+C, H, ROUNDS = 320, 160, 3
+MASK = [1, 2, 3]
+U8, F8, BF, F32, I32, U16 = "uint8", "float8_e4m3fn_x4", "bfloat16", "float32", "int32", "uint16"
+BY_PRODUCT = 4
+
+SCRATCH = {}
+
+
+def _sb(name, cols, dtype):
+    SCRATCH[name] = ("sbuf", [128, cols], dtype)
+
+
+def _mx(name, cols):
+    _sb(name, cols, F8)
+    _sb(name + "s", cols, U8)
+
+
+for _k in range(8):
+    SCRATCH["ps%d" % _k] = ("psum", [128, 512], F32)
+for _n, _w in (("xin", 1280), ("xn", 1280), ("ut", 512), ("vt", 512), ("ones", 1024), ("zt", 1280), ("hb", 320), ("eqt", 640), ("zs", 1280),
+               ("fs", 528), ("dat", 320), ("wn", 2560), ("wt", 10240), ("wv", 10240), ("gt", 640), ("ft", 640), ("at", 640),
+               ("bt", 640), ("vb", 640), ("m16", 320), ("m32", 320), ("est", 2048), ("cst", 4096), ("cc1", 1024), ("cci", 640), ("sgn", 512),
+               ("sg2", 512), ("gm", 8)):
+    _sb(_n, _w, BF)
+for _k in range(6):
+    _sb("ct%d" % _k, 1280, BF)
+    _mx("cq%d" % _k, 320)
+for _n, _w in (("tr", 320), ("ob", 640), ("su", 80), ("sg", 80), ("st", 96), ("r1", 80), ("r0", 80), ("dg", 80), ("n2f", 32),
+               ("vf", 32), ("vtr", 32), ("om", 512), ("jj", 640), ("sc", 32), ("gi", 8), ("pl", 20), ("s2", 20), ("sz", 20), ("it", 20),
+               ("smk", 80), ("z80", 80), ("yo", 320)):
+    _sb(_n, _w, F32)
+for _n, _w in (("pi", 8), ("lui", 64), ("li", 480)):
+    _sb(_n, _w, I32)
+for _n, _w in (("lu", 64), ("pos", 32), ("off", 32), ("wl", 32)):
+    _sb(_n, _w, U16)
+for _n, _w in (("xq", 320), ("uq", 128), ("us", 384), ("vq", 128), ("wq", 512), ("er", 1024), ("kc", 1024), ("k1", 256), ("ki", 160),
+               ("fq", 132), ("nq", 640), ("gq", 160), ("fqq", 160), ("aq", 160), ("bq", 160)):
+    _mx(_n, _w)
+for _k in range(ROUNDS):
+    _mx("gl%d" % _k, 160)
+    _mx("bl%d" % _k, 160)
+
+SEMAPHORES = ["ev", "ea", "et", "ep"] + ["d%d" % _k for _k in range(80)]
+for _k in range(ROUNDS):
+    SEMAPHORES += ["ga%d" % _k, "ba%d" % _k, "gs%d" % _k, "bs%d" % _k]
+
+
+def rank_program(g, core, T, topo):
+    rank = T.rank_of(core)
+    if rank is None:
+        return
+    queue = {"v": g.vector, "a": g.scalar, "t": g.tensor, "p": g, "s": g.sync}
+    known = {q: {} for q in queue}
+    count, snaps, log, ndma, final = {}, {}, {}, [0], {}
+
+    def A(name, a, b, step=1):
+        return (name, a, b, step)
+
+    def ap(s):
+        return T[s[0]][:, s[1]:s[2]] if s[3] == 1 else T[s[0]][:, s[1]:s[2]:s[3]]
+
+    def hit(x, y):
+        return x[1] < y[2] and y[1] < x[2] and (x[1] - y[1]) % math.gcd(x[3], y[3]) == 0
+
+    def need(q, tokens):
+        for tok in sorted(set(tokens), key=lambda k: (k[0], -k[1])):
+            if known[q].get(tok[0], 0) < tok[1]:
+                queue[q].wait_ge(T.sem[tok[0]], tok[1])
+                known[q][tok[0]] = tok[1]
+                for s, n in snaps[tok].items():
+                    known[q][s] = max(known[q].get(s, 0), n)
+
+    def note(s, w, q, token, loose=False):
+        keep = []
+        for r in log.get(s[0], []):
+            x = r[0]
+            inside = s[1] <= x[1] and x[2] <= s[2] and (s[3] == 1 or (s[3] == x[3] and (s[1] - x[1]) % s[3] == 0))
+            if loose or not (inside and (w or (r[2] == q and not r[1]))):
+                keep.append(r)
+        keep.append((s, w, q, token, loose))
+        log[s[0]] = keep
+
+    def emit(q, fn, outs, ins, token=None, acc=False, loose=False):
+        tokens = []
+        for lst, w in ((ins, False), (outs, True)):
+            for s in lst:
+                bank = s[0][:2] == "ps"
+                for r in log.get(s[0], ()):
+                    if bank:
+                        if not (r[2] == q and (acc or not (w or r[1]))):
+                            tokens.append(r[3])
+                    elif loose and w and r[1] and r[2] == q and r[4]:
+                        continue
+                    elif (w or r[1]) and hit(s, r[0]):
+                        tokens.append(r[3])
+        need(q, tokens)
+        inst = fn()
+        if token is None:
+            name = "e" + q
+            count[name] = count.get(name, 0) + 1
+            token = (name, count[name])
+            inst.then_inc(T.sem[name], 1)
+        final[token[0]] = token[1]
+        snaps[token] = dict(known[q])
+        for s in ins:
+            note(s, False, q, token, q == "s")
+        for s in outs:
+            note(s, True, q, token, loose)
+
+    def dma(q, out_ap, in_ap, outs, ins, loose=False):
+        tok = ("d%d" % ndma[0], 16)
+        ndma[0] += 1
+        emit(q, lambda: queue[q].dma_start(out_ap, in_ap).then_inc(T.sem[tok[0]], 16), outs, ins, tok, loose=loose)
+
+    def memset(s, c):
+        emit("v", lambda: g.vector.memset(ap(s), c), [s], [])
+
+    def copy(o, i):
+        emit("v", lambda: g.vector.tensor_copy(ap(o), ap(i)), [o], [i])
+
+    def tt(o, a, b, op):
+        emit("v", lambda: g.vector.tensor_tensor(ap(o), ap(a), ap(b), op), [o], [a, b])
+
+    def ts(o, a, c1, c2, op0, op1=None):
+        ins = [a] + [c for c in (c1, c2) if isinstance(c, tuple)]
+        x1 = ap(c1) if isinstance(c1, tuple) else c1
+        x2 = ap(c2) if isinstance(c2, tuple) else c2
+        if op1 is None:
+            emit("v", lambda: g.vector.tensor_scalar(ap(o), ap(a), x1, None, op0), [o], ins)
+        else:
+            emit("v", lambda: g.vector.tensor_scalar(ap(o), ap(a), x1, x2, op0, op1), [o], ins)
+
+    def scan(o, a, b, init, op0, op1):
+        emit("v", lambda: g.vector.tensor_tensor_scan(ap(o), ap(a), ap(b), init, op0, op1), [o], [a, b])
+
+    def act(o, i, fn, bias=None, scale=1.0):
+        if bias is None:
+            emit("a", lambda: g.scalar.activation(ap(o), ap(i), fn, scale=scale), [o], [i])
+        elif isinstance(bias, tuple):
+            emit("a", lambda: g.scalar.activation(ap(o), ap(i), fn, bias=ap(bias), scale=scale), [o], [i, bias])
+        else:
+            emit("a", lambda: g.scalar.activation(ap(o), ap(i), fn, bias=bias, scale=scale), [o], [i])
+
+    def quant(o, c, n, i, c2):
+        src = A(i, c2, c2 + 4 * n)
+        emit("v", lambda: g.vector.quantize_mx(T[o][:, c:c + n], T[o + "s"][:, c:c + n], ap(src)), [A(o, c, c + n), A(o + "s", c, c + n)], [src])
+
+    def mm(bank, w, wc, x, xc, n, start=True, stop=True):
+        o = A("ps%d" % bank, 0, 512)
+        emit("t", lambda: g.tensor.matmul_mx(T["ps%d" % bank][:, 0:n], T[w][:, wc:wc + 128], T[w + "s"][:, wc:wc + 128],
+                                             T[x][:, xc:xc + n], T[x + "s"][:, xc:xc + n], start, stop),
+             [o], [A(w, wc, wc + 128), A(w + "s", wc, wc + 128), A(x, xc, xc + n), A(x + "s", xc, xc + n)], acc=not start)
+
+    def P(bank, n, a=0):
+        return A("ps%d" % bank, a, n)
+
+    def gather(q, o, win, lst):
+        if q == "v":
+            emit("v", lambda: g.vector.tensor_copy(ap(o), ap(win).indirect(ap(lst))), [o], [win, lst])
+        else:
+            emit("a", lambda: g.scalar.activation(ap(o), ap(win).indirect(ap(lst)), Fn.Copy), [o], [win, lst])
+
+    def send(dst, src, land, sem, done):
+        rid, pid, _ = topo.addr(dst)
+        eng = topo.engines(core, dst)
+        ec, es = eng[0::2], eng[1::4]
+        total = len(ec) + len(es)
+        need("p", [r[3] for nm in (src, src + "s") for r in log[nm] if r[1]])
+        g.remote_dma(T[land][:, 0:H].bitcast(dt.uint8), T[src][:, 0:H].bitcast(dt.uint8), T.sem[sem], T.sem[done], pid, rid, sum(1 << e for e in ec))
+        g.remote_dma(T[land + "s"][:, 0:H], T[src + "s"][:, 0:H], T.sem[sem], T.sem[done], pid, rid, sum(1 << e for e in es))
+        tok, arr = (done, total), (sem, total)
+        snaps[tok], snaps[arr] = dict(known["p"]), {}
+        final[done], final[sem] = total, total
+        for nm in (src, src + "s"):
+            note(A(nm, 0, H), False, "p", tok)
+        for nm in (land, land + "s"):
+            log[nm] = [(A(nm, 0, H), True, "r", arr, False)]
+
+    def iota(o, pattern, base, cm):
+        if o[0] in ("pi", "lui"):
+            emit("p", lambda: g.iota(ap(o), pattern, base, cm), [o], [])
+        else:
+            emit("p", lambda: g.iota(ap(o), pattern, base, cm, allow_small_or_imprecise_dtypes=True), [o], [])
+
+    def select_e(b):
+        o, i = A("est", 512 * b, 512 * b + 512), A("ones", 0, 512)
+        emit("p", lambda: g.affine_select(ap(o), ap(i), [[-1, 128], [1000, 4]], Op.is_equal, 0.0, -1000 * b, 1), [o], [i])
+
+    def turn(b):
+        quant("er", 256 * b, 128, "est", 512 * b)
+        quant("er", 256 * b + 128, 128, "est", 512 * b)
+
+    def pcol(k):
+        return A("pi", k, k + 1)
+
+    def col(k):
+        return A("sc", k, k + 1)
+
+    dma("a", T.ut[:, :], T.u[:, :], [A("ut", 0, 512)], [])
+    dma("s", T.xin[:, :], T.x[:, :], [A("xin", 0, 1280)], [])
+    dma("s", T.wq[:, :].bitcast(dt.uint8), T.wc[:, :], [A("wq", 0, 512)], [])
+    dma("s", T.wqs[:, :], T.ws[:, :], [A("wqs", 0, 512)], [])
+    dma("s", T.vt[:, :], T.v[:, :], [A("vt", 0, 512)], [])
+
+    memset(A("ones", 0, 1024), 1.0)
+    iota(A("lui", 0, 8), [[16, 8]], 0, 0)
+    iota(A("lui", 8, 16), [[32, 4], [0, 2]], 0, 0)
+    iota(A("lui", 16, 24), [[32, 4], [0, 2]], 16, 0)
+    iota(A("lui", 24, 44), [[32, 10], [0, 2]], 0, 0)
+    iota(A("lui", 44, 64), [[32, 10], [0, 2]], 16, 0)
+    iota(A("pi", 0, 1), [[0, 1]], 0, 1)
+    for b in range(4):
+        select_e(b)
+    iota(A("om", 0, 512), [[1, 8], [8, 16], [0, 4]], 0, 0)
+    iota(A("gi", 0, 8), [[1, 8]], 0, 0)
+    iota(A("jj", 320, 640), [[0, 10], [1, 32]], 0, 0)
+    iota(A("jj", 0, 320), [[0, 20], [1, 16]], 0, 0)
+    iota(A("smk", 0, 80), [[0, 20], [1, 4]], 0, 0)
+    iota(A("pl", 0, 20), [[128, 20]], 0, 0)
+    iota(A("s2", 0, 20), [[0, 2], [512, 5], [16, 2]], 0, 0)
+
+    def fill(s, c):
+        act(s, A("ones", 0, len(range(s[1], s[2], s[3]))), Fn.Copy, scale=c)
+
+    fill(A("zt", 0, 1024), 0.0)
+    fill(A("zt", 1024, 1280), 0.0)
+
+    copy(A("lu", 0, 64), A("lui", 0, 64))
+    memset(A("cc1", 0, 1024), 0.0)
+    for a in range(4):
+        for e in range(4):
+            m = 32 * a + 16 * (e // 2)
+            s = A("cc1", 4 * m + e, 4 * (m + 16), 4)
+            emit("v", lambda: g.vector.memset(T.cc1[32 * a:32 * a + 32, s[1]:s[2]:4], 1.0), [s], [], loose=True)
+    ts(pcol(1), pcol(0), 15, None, Op.bitwise_and)
+    ts(pcol(2), pcol(0), 31, None, Op.bitwise_and)
+    ts(pcol(3), pcol(0), 4, None, Op.arith_shift_right)
+    ts(A("cc1", 512, 1024), A("cc1", 0, 512), 0.5, None, Op.mult)
+    quant("k1", 0, 256, "cc1", 0)
+    copy(A("sc", 0, 3), A("pi", 1, 4))
+    quant("uq", 0, 128, "ut", 0)
+    lst = A("lu", 0, 24)
+    emit("a", lambda: g.scalar.activation(T.uss[:, 0:384], T.uqs[:, 0:128].indirect(ap(lst)), Fn.Copy), [A("uss", 0, 384)], [A("uqs", 0, 128), lst])
+    emit("v", lambda: g.vector.tensor_copy(T.us[:, 0:384].bitcast(dt.uint32), T.uq[:, 0:128].bitcast(dt.uint32).indirect(ap(lst))),
+         [A("us", 0, 384)], [A("uq", 0, 128), lst])
+    fill(A("ct5", 0, 1024), 0.0)
+    fill(A("ct5", 1024, 1280), 0.0)
+    ts(col(3), col(0), 8.0, col(2), Op.mult, Op.add)
+    ts(col(4), col(3), -1.0, -0.5, Op.mult, Op.add)
+    ts(col(5), col(3), -1.0, None, Op.mult)
+    ts(col(18), col(0), -1.0, None, Op.mult)
+
+    def consts_a():
+        act(A("sgn", 0, 512), A("om", 0, 512), Fn.Sign, bias=col(4))
+        act(A("cst", 0, 512), A("sgn", 0, 512), Fn.Relu, scale=2.0)
+        act(A("cst", 512, 1024), A("sgn", 0, 512), Fn.Relu, scale=-2.0)
+        act(A("sg2", 0, 512), A("om", 0, 512), Fn.Abs, bias=col(5))
+        act(A("cst", 1024, 1536), A("sg2", 0, 512), Fn.Relu, bias=2.0, scale=-2.0)
+        fill(A("cst", 1536, 2048), 2.0)
+        fill(A("cst", 2048, 3072), 0.0)
+        fill(A("cst", 3072, 4096), 0.0)
+        for b in range(4):
+            for e in range(b + 1):
+                s = A("cst", 2048 + 512 * b + 4 * (3 + e // 2) + e, 2048 + 512 * b + 512, 64)
+                if e < b:
+                    fill(s, 2.0)
+                else:
+                    act(s, A("gm", 0, 8), Fn.Copy)
+        fill(A("cci", 0, 640), 0.0)
+        for e, c in ((80, -1.0), (86, -1.0), (121, 1.0), (127, 1.0)):
+            fill(A("cci", e, e + 1), c)
+        act(A("eqt", 0, 320), A("jj", 0, 320), Fn.Abs, bias=col(18))
+        act(A("m16", 0, 320), A("eqt", 0, 320), Fn.Relu, bias=1.0, scale=-1.0)
+        act(A("smk", 0, 80), A("smk", 0, 80), Fn.Sign)
+        fill(A("z80", 0, 80), 0.0)
+        fill(A("st", 0, 8), 0.0)
+        fill(A("vf", 0, 32), 0.0)
+        fill(A("fs", 0, 528), 0.0)
+
+    def consts_v():
+        none, big, small = 1.5 * 2.0 ** 35, 1.5 * 2.0 ** 30, 1.5 * 2.0 ** 26
+        ts(col(8), col(0), 3.0, none, Op.is_ge, Op.mult)
+        for k, v in ((9, big), (10, small)):
+            ts(col(k), col(0), float(k - 9), v, Op.is_equal, Op.mult)
+        for k, v in ((11, none), (12, big), (13, small)):
+            ts(col(k), col(0), float(k - 11), v, Op.is_equal, Op.mult)
+        ts(col(14), col(2), 2.0, None, Op.mult)
+        tt(col(19), col(8), col(9), Op.add)
+        tt(col(20), col(8), col(11), Op.add)
+        tt(col(21), col(12), col(13), Op.add)
+        ts(col(15), col(0), 32.0, col(14), Op.mult, Op.add)
+        ts(col(16), col(2), -1.0, 8.0, Op.mult, Op.add)
+        tt(col(6), col(19), col(10), Op.add)
+        tt(col(7), col(20), col(21), Op.add)
+        ts(A("s2", 0, 20), A("s2", 0, 20), col(15), None, Op.add)
+        ts(col(17), col(2), -2.0, 16.0, Op.mult, Op.add)
+        ts(A("pl", 0, 20), A("pl", 0, 20), col(3), 0.5, Op.add, Op.add)
+        ts(A("sz", 0, 20), A("s2", 0, 20), col(16), None, Op.add)
+        quant("kc", 0, 512, "cst", 0)
+        quant("kc", 512, 512, "cst", 2048)
+        quant("ki", 0, 160, "cci", 0)
+
+    flip = [0]
+
+    def other():
+        flip[0] += 1
+        return "va"[flip[0] % 2]
+
+    def unpack(pair, b, d, bank, q, i):
+        mm(bank, "er", 256 * b + 16 * d, pair, 0, H)
+        o = A("wv", 2560 * b + 2 * d + i, 2560 * b + 2560, 16)
+        if q == "v":
+            copy(o, P(bank, H))
+        else:
+            act(o, P(bank, H), Fn.Copy)
+
+    def layer(pair, tile, out):
+        for b in range(4):
+            mm(b, "wq", 128 * b, pair, 0, H)
+        for b in range(4):
+            o = A(tile, b, 4 * H, 4)
+            if b % 2 == 0:
+                ts(o, P(b, H), 0.0, 0.03125, Op.max, Op.mult)
+            else:
+                act(o, P(b, H), Fn.Relu, scale=0.03125)
+        quant(out, 0, H, tile, 0)
+
+    def L(k):
+        return A("li", 20 * k, 20 * k + 20)
+
+    def TW(b):
+        return A("wt", 320 * b, 320 * b + 9280)
+
+    for rd in range(ROUNDS):
+        dst = T.cores[rank ^ MASK[rd]]
+        dma("s", T.wn[:, 0:1280], T.zt[:, :], [A("wn", 0, 1280)], [A("zt", 0, 1280)])
+        dma("s", T.wn[:, 1280:2560], T.zt[:, :], [A("wn", 1280, 2560)], [A("zt", 0, 1280)])
+        quant("xq", 0, C, "xin" if rd == 0 else "xn", 0)
+        for bank, k in ((0, 0), (1, 1), (2, 2), (4, 1), (5, 2)):
+            mm(bank, "us", 128 * k, "xq", 0, C)
+        emit("v", lambda: g.vector.transpose(T.tr[:, 0:320], T.ps0[:, 0:320]), [A("tr", 0, 320)], [P(0, 320)])
+
+        def own(gg, b):
+            return A("tr", 32 * b + 16 * gg, 32 * b + 16 * gg + 1)
+
+        def t_number(b, d):
+            bank = 6 + b % 2
+            mm(bank, "er", 256 * b + 16 * d, "xq", 0, C)
+            act(A("wt", 1280 * d + 320 * b, 1280 * d + 320 * b + 320), P(bank, C), Fn.Copy)
+
+        def turns_by_dma():
+            for d in range(BY_PRODUCT, 8):
+                o, i, k = A("wt", 1280 * d, 1280 * d + 1280), A("wt", 0, 1280), 128 - 16 * d
+                dma("s", T.wt[0:k, o[1]:o[2]], T.wt[16 * d:128, 0:1280], [o], [i], loose=True)
+                dma("s", T.wt[k:128, o[1]:o[2]], T.wt[0:16 * d, 0:1280], [o], [i], loose=True)
+
+        def passes(t):
+            for gg, b in ((0, 2 * t), (0, 2 * t + 1), (1, 2 * t), (1, 2 * t + 1)):
+                e, lo = 2 * gg + b % 2, 32 * b + 32
+                ts(A("ct%d" % t, e, 4 * lo, 4), P(1 + gg, lo), own(gg, b), None, Op.is_lt)
+                if lo < C:
+                    ts(A("ct%d" % t, 4 * lo + e, 1280, 4), P(1 + gg, C, lo), own(gg, b), None, Op.is_le)
+
+        def passes_a(t):
+            for k, (gg, b) in enumerate(((0, 2 * t), (0, 2 * t + 1), (1, 2 * t), (1, 2 * t + 1))):
+                e, lo, z = 2 * gg + b % 2, 32 * b + 32, 320 * k
+                act(A("zs", z, z + C), P(4 + gg, C), Fn.Sign, bias=own(gg, b), scale=-1.0)
+                act(A("ct%d" % t, e, 4 * lo, 4), A("zs", z, z + lo), Fn.Sign, bias=-0.5)
+                if lo < C:
+                    act(A("ct%d" % t, 4 * lo + e, 1280, 4), A("zs", z + lo, z + C), Fn.Sign, bias=0.5)
+
+        def add_ranks(t, w, start, stop):
+            quant("cq%d" % t, 0, C, "ct%d" % t, 0)
+            mm(3, "k1", w, "cq%d" % t, 0, C, start=start, stop=stop)
+
+        for k in range(2):
+            gather("a", A("ob", 320 * k, 320 * k + 320), A("tr", 0, 320), A("lu", 24 + 20 * k, 44 + 20 * k))
+        if rd == 0:
+            turn(0)
+            passes(0)
+            for b in range(1, 4):
+                turn(b)
+            ts(A("gm", 0, 8), A("gi", 0, 8), col(2), 2.0, Op.is_gt, Op.mult)
+        for b in range(4):
+            t_number(b, 0)
+        turns_by_dma()
+        passes_a(4)
+        if rd == 0:
+            consts_a()
+        else:
+            passes(0)
+        add_ranks(0, 0, True, False)
+        passes(1)
+        add_ranks(1, 0, False, False)
+        for b in range(4):
+            t_number(b, 1)
+        if rd == 0:
+            ts(A("m32", 0, 320), A("jj", 320, 640), col(1), None, Op.is_gt)
+        passes(2)
+        add_ranks(2, 0, False, False)
+        for gg in range(2):
+            o = A("eqt", 320 * gg, 320 * gg + 320)
+            tt(o, P(1 + gg, C), A("ob", 320 * gg, 320 * gg + 320), Op.is_equal)
+            tt(A("ct5", 2 * gg, 1280, 4), o, A("m32", 0, 320), Op.mult)
+        add_ranks(5, 0, False, False)
+        add_ranks(4, 128, False, False)
+        for b in range(4):
+            t_number(b, 2)
+        passes(3)
+        add_ranks(3, 0, False, True)
+        if rd == 0:
+            consts_v()
+        ts(A("hb", 0, 320), P(3, C), 128.0, 0.5, Op.is_lt, Op.subtract)
+        tt(A("fs", 16, 336), A("hb", 0, 320), A("m16", 0, 320), Op.mult)
+        quant("fq", 0, 132, "fs", 0)
+        mm(0, "kc", 0, "fq", 4, 128, True, False)
+        mm(0, "kc", 128, "fq", 0, 128, False, True)
+        mm(1, "kc", 256, "fq", 4, 128)
+        mm(2, "kc", 384, "fq", 4, 128)
+        mm(4, "kc", 512, "fq", 4, 128)
+        mm(5, "kc", 640, "fq", 4, 128)
+        mm(3, "kc", 768, "fq", 4, 128)
+        scan(A("su", 0, 80), P(0, 80), A("z80", 0, 80), -0.5, Op.add, Op.add)
+        mm(0, "kc", 896, "fq", 4, 128)
+        for b in range(4):
+            t_number(b, 3)
+        scan(A("sg", 0, 80), A("smk", 0, 80), P(1, 80), 0.0, Op.mult, Op.add)
+        scan(A("st", 8, 88), P(2, 80), A("z80", 0, 80), 0.0, Op.add, Op.add)
+        n2, y, h2 = L(0), L(1), L(2)
+        tt(A("n2f", 0, 20), A("su", 3, 80, 4), A("sg", 3, 80, 4), Op.mult)
+        ts(A("r1", 0, 80), A("st", 7, 87), col(6), col(6), Op.add, Op.subtract)
+        tt(n2, A("n2f", 0, 20), A("pl", 0, 20), Op.add)
+        ts(A("r0", 0, 80), A("st", 7, 87), col(7), col(7), Op.add, Op.subtract)
+        ts(y, n2, 4, 31, Op.arith_shift_right, Op.bitwise_and)
+        ts(h2, n2, 14, None, Op.bitwise_and)
+        tt(A("dg", 0, 80), A("r1", 0, 80), A("r0", 0, 80), Op.subtract)
+        ts(L(3), y, -14, None, Op.mult)
+        ts(L(4), h2, 31, None, Op.mult)
+        for b, bank in ((0, 4), (1, 5)):
+            tt(A("dat", b, 320, 4), P(bank, 80), A("dg", 0, 80), Op.add)
+        tt(L(5), L(3), n2, Op.add)
+        tt(A("dat", 2, 320, 4), P(3, 80), A("dg", 0, 80), Op.add)
+        tt(L(6), L(5), L(4), Op.add)
+        tt(A("dat", 3, 320, 4), P(0, 80), A("dg", 0, 80), Op.add)
+        copy(A("pos", 0, 20), L(6))
+        slots, lst = A("wn", 0, 2560), A("pos", 0, 20)
+        emit("v", lambda: g.vector.tensor_copy(ap(slots).indirect(ap(lst)), T.dat[:, 0:320]), [slots], [lst, A("dat", 0, 320)])
+        quant("nq", 0, 320, "wn", 0)
+        quant("nq", 320, 320, "wn", 1280)
+        for s in range(5):
+            mm(1, "nq", 128 * s, "ki", 20 - 2 * s, 128, s == 0, s == 4)
+        tt(L(7), P(1, 20), A("sz", 0, 20), Op.add)
+        tt(L(8), P(1, 20), A("s2", 0, 20), Op.add)
+        ts(L(9), L(7), 7, None, Op.bitwise_and)
+        ts(L(10), L(8), 3, None, Op.arith_shift_right)
+        ts(L(21), L(9), 1280, None, Op.mult)
+        tt(L(11), L(21), L(10), Op.add)
+        copy(A("off", 0, 20), L(11))
+        for b in range(4):
+            gather("va"[b % 2], A("gt", b, 640, 4), TW(b), A("off", 10, 20))
+        quant("gq", 0, H, "gt", 0)
+        send(dst, "gq", "gl%d" % rd, "ga%d" % rd, "gs%d" % rd)
+        for b in range(4):
+            gather("va"[b % 2], A("ft", b, 640, 4), TW(b), A("off", 0, 10))
+        quant("fqq", 0, H, "ft", 0)
+        layer("fqq", "at", "aq")
+        turns = [(b, d) for b in range(4) for d in range(8)]
+        for k, (b, d) in enumerate(turns[:8]):
+            unpack("aq", b, d, 4 + k % 4, other(), 0)
+        layer("gl%d" % rd, "bt", "bq")
+        send(dst, "bq", "bl%d" % rd, "ba%d" % rd, "bs%d" % rd)
+        for k, (b, d) in enumerate(turns[8:]):
+            unpack("aq", b, d, 4 + k % 4, other(), 0)
+        ts(L(12), n2, 16, None, Op.bitwise_and)
+        ts(L(13), y, -8, None, Op.mult)
+        ts(L(14), n2, col(17), None, Op.add)
+        ts(L(15), L(12), 15.5, None, Op.mult)
+        tt(L(16), n2, L(13), Op.add)
+        ts(L(17), L(14), 14, None, Op.bitwise_and)
+        tt(L(18), L(16), L(15), Op.add)
+        tt(L(19), L(17), h2, Op.subtract)
+        tt(L(20), L(18), L(19), Op.add)
+        copy(A("wl", 0, 20), L(20))
+        if rd == 0:
+            quant("vq", 0, 128, "vt", 0)
+        if rd == ROUNDS - 1:
+            ts(A("r0", 0, 20), A("sg", 3, 80, 4), -639.75, None, Op.mult)
+            ts(A("r1", 0, 20), A("n2f", 0, 20), 0.5, 639.75, Op.mult, Op.add)
+            ts(A("it", 0, 20), A("pl", 0, 20), 0.5, None, Op.mult)
+            tt(A("dg", 0, 20), A("r0", 0, 20), A("r1", 0, 20), Op.add)
+            tt(A("vf", 0, 20), A("dg", 0, 20), A("it", 0, 20), Op.add)
+            emit("v", lambda: g.vector.transpose(T.vtr[:, 0:32], T.vf[:, 0:32]), [A("vtr", 0, 32)], [A("vf", 0, 32)])
+            for k in range(8):
+                a, o = k // 2, 16 * (k % 2)
+                dma("s", T.op[k:k + 1, :], T.vtr[32 * a:32 * a + 20, o:o + 16], [], [A("vtr", 0, 32)])
+
+        def add_gathered(b, a, n):
+            o, win, t2 = A("xn", 4 * a + b, 4 * (a + n), 4), A("wv", 2560 * b, 2560 * b + 2560), A("wt", 320 * b + a, 320 * b + a + n)
+            li = A("wl", a // 16, (a + n) // 16)
+            emit("v", lambda: g.vector.tensor_tensor(ap(o), ap(win).indirect(ap(li)), ap(t2), Op.add), [o], [win, li, t2])
+
+        def gather_v(b, slot, a, n):
+            gather("a", A("vb", 320 * slot + a, 320 * slot + a + n), A("wv", 2560 * b, 2560 * b + 2560), A("wl", a // 16, (a + n) // 16))
+
+        def add_v(b, slot, a, n):
+            tt(A("xn", 4 * a + b, 4 * (a + n), 4), A("vb", 320 * slot + a, 320 * slot + a + n), A("wt", 320 * b + a, 320 * b + a + n), Op.add)
+
+        land = "bl%d" % rd
+        for b in range(4):
+            for d in range(8):
+                unpack(land, b, d, d, other(), 1)
+            if b == 1:
+                add_gathered(0, 0, 320)
+            if b == 2:
+                gather_v(1, 0, 0, 320)
+        gather_v(2, 1, 0, 320)
+        add_v(1, 0, 0, 320)
+        add_gathered(3, 0, 160)
+        gather_v(3, 0, 160, 160)
+        add_v(2, 1, 0, 320)
+        add_v(3, 0, 160, 160)
+
+    quant("xq", 0, C, "xn", 0)
+    dma("s", T.oc[:, :], T.xq[:, 0:C].bitcast(dt.uint8), [], [A("xq", 0, C)])
+    mm(0, "vq", 0, "xq", 0, C)
+    for k in range(4):
+        dma("a", T.osc[4 * k:4 * k + 4, :], T.xqs[32 * k:32 * k + 4, 0:C], [], [A("xqs", 0, C)])
+    copy(A("yo", 0, C), P(0, C))
+    dma("s", T.y[:, :], T.yo[:, 0:C], [], [A("yo", 0, C)])
+    for s in sorted(final):
+        if known["p"].get(s, 0) < final[s]:
+            g.wait_ge(T.sem[s], final[s])

@@ -4,7 +4,8 @@ from concourse.mybir import dt, AluOpType as Op, ActivationFunctionType as Fn
 C, H, ROUNDS = 320, 160, 3
 MASK = [1, 2, 3]
 U8, F8, BF, F32, I32, U16 = "uint8", "float8_e4m3fn_x4", "bfloat16", "float32", "int32", "uint16"
-BY_PRODUCT = 4
+T_PRODUCTS, A_PRODUCTS = 4, 4
+BY_SCALAR = [8, 9]
 
 SCRATCH = {}
 
@@ -22,28 +23,27 @@ for _k in range(8):
     SCRATCH["ps%d" % _k] = ("psum", [128, 512], F32)
 for _n, _w in (("xin", 1280), ("xn", 1280), ("ut", 512), ("vt", 512), ("ones", 1024), ("zt", 1280), ("hb", 320), ("eqt", 640), ("zs", 1280),
                ("fs", 528), ("dat", 320), ("wn", 2560), ("wt", 10240), ("wv", 10240), ("gt", 640), ("ft", 640), ("at", 640),
-               ("bt", 640), ("vb", 640), ("m16", 320), ("m32", 320), ("est", 2048), ("cst", 4096), ("cc1", 1024), ("cci", 640), ("sgn", 512),
-               ("sg2", 512), ("gm", 8)):
+               ("bt", 640), ("vb", 640), ("m16", 320), ("m32", 320), ("est", 2048), ("cst", 4096), ("cc1", 1024), ("cci", 640), ("two", 8)):
     _sb(_n, _w, BF)
 for _k in range(6):
     _sb("ct%d" % _k, 1280, BF)
     _mx("cq%d" % _k, 320)
 for _n, _w in (("tr", 320), ("ob", 640), ("su", 80), ("sg", 80), ("st", 96), ("r1", 80), ("r0", 80), ("dg", 80), ("n2f", 32),
-               ("vf", 32), ("vtr", 32), ("om", 512), ("jj", 640), ("sc", 32), ("gi", 8), ("pl", 20), ("s2", 20), ("sz", 20), ("it", 20),
-               ("smk", 80), ("z80", 80), ("yo", 320)):
+               ("vf", 32), ("vtr", 32), ("om", 512), ("jj", 640), ("sc", 32), ("pl", 20), ("s2", 20), ("sz", 20), ("it", 20),
+               ("smk", 80), ("z80", 80), ("yo", 320), ("lf", 200)):
     _sb(_n, _w, F32)
 for _n, _w in (("pi", 8), ("lui", 64), ("li", 480)):
     _sb(_n, _w, I32)
 for _n, _w in (("lu", 64), ("pos", 32), ("off", 32), ("wl", 32)):
     _sb(_n, _w, U16)
-for _n, _w in (("xq", 320), ("uq", 128), ("us", 384), ("vq", 128), ("wq", 512), ("er", 1024), ("kc", 1024), ("k1", 256), ("ki", 160),
-               ("fq", 132), ("nq", 640), ("gq", 160), ("fqq", 160), ("aq", 160), ("bq", 160)):
+for _n, _w in (("xq", 320), ("uq", 128), ("us", 384), ("vq", 128), ("wq", 512), ("e0", 512), ("er", 1024), ("kc", 1024), ("k1", 256),
+               ("ki", 160), ("fq", 132), ("nq", 640), ("gq", 160), ("fqq", 160), ("aq", 160), ("bq", 160)):
     _mx(_n, _w)
 for _k in range(ROUNDS):
     _mx("gl%d" % _k, 160)
     _mx("bl%d" % _k, 160)
 
-SEMAPHORES = ["ev", "ea", "et", "ep"] + ["d%d" % _k for _k in range(80)]
+SEMAPHORES = ["ev", "ea", "et", "ep"] + ["d%d" % _k for _k in range(120)]
 for _k in range(ROUNDS):
     SEMAPHORES += ["ga%d" % _k, "ba%d" % _k, "gs%d" % _k, "bs%d" % _k]
 
@@ -185,13 +185,8 @@ def rank_program(g, core, T, topo):
         else:
             emit("p", lambda: g.iota(ap(o), pattern, base, cm, allow_small_or_imprecise_dtypes=True), [o], [])
 
-    def select_e(b):
-        o, i = A("est", 512 * b, 512 * b + 512), A("ones", 0, 512)
-        emit("p", lambda: g.affine_select(ap(o), ap(i), [[-1, 128], [1000, 4]], Op.is_equal, 0.0, -1000 * b, 1), [o], [i])
-
-    def turn(b):
-        quant("er", 256 * b, 128, "est", 512 * b)
-        quant("er", 256 * b + 128, 128, "est", 512 * b)
+    def select(o, i, pattern, cmp, base, cm):
+        emit("p", lambda: g.affine_select(ap(o), ap(i), pattern, cmp, 0.0, base, cm), [o], [i])
 
     def pcol(k):
         return A("pi", k, k + 1)
@@ -199,88 +194,84 @@ def rank_program(g, core, T, topo):
     def col(k):
         return A("sc", k, k + 1)
 
+    def fill(s, c):
+        act(s, A("ones", 0, len(range(s[1], s[2], s[3]))), Fn.Copy, scale=c)
+
     dma("a", T.ut[:, :], T.u[:, :], [A("ut", 0, 512)], [])
     dma("s", T.xin[:, :], T.x[:, :], [A("xin", 0, 1280)], [])
     dma("s", T.wq[:, :].bitcast(dt.uint8), T.wc[:, :], [A("wq", 0, 512)], [])
     dma("s", T.wqs[:, :], T.ws[:, :], [A("wqs", 0, 512)], [])
     dma("s", T.vt[:, :], T.v[:, :], [A("vt", 0, 512)], [])
 
-    memset(A("ones", 0, 1024), 1.0)
+    memset(A("ones", 0, 512), 1.0)
+    iota(A("pi", 0, 1), [[0, 1]], 0, 1)
     iota(A("lui", 0, 8), [[16, 8]], 0, 0)
     iota(A("lui", 8, 16), [[32, 4], [0, 2]], 0, 0)
     iota(A("lui", 16, 24), [[32, 4], [0, 2]], 16, 0)
-    iota(A("lui", 24, 44), [[32, 10], [0, 2]], 0, 0)
-    iota(A("lui", 44, 64), [[32, 10], [0, 2]], 16, 0)
-    iota(A("pi", 0, 1), [[0, 1]], 0, 1)
     for b in range(4):
-        select_e(b)
+        select(A("est", 512 * b, 512 * b + 512), A("ones", 0, 512), [[-1, 128], [1000, 4]], Op.is_equal, -1000 * b, 1)
+        if b == 0:
+            iota(A("lui", 24, 44), [[32, 10], [0, 2]], 0, 0)
+            iota(A("lui", 44, 64), [[32, 10], [0, 2]], 16, 0)
     iota(A("om", 0, 512), [[1, 8], [8, 16], [0, 4]], 0, 0)
-    iota(A("gi", 0, 8), [[1, 8]], 0, 0)
     iota(A("jj", 320, 640), [[0, 10], [1, 32]], 0, 0)
     iota(A("jj", 0, 320), [[0, 20], [1, 16]], 0, 0)
     iota(A("smk", 0, 80), [[0, 20], [1, 4]], 0, 0)
     iota(A("pl", 0, 20), [[128, 20]], 0, 0)
     iota(A("s2", 0, 20), [[0, 2], [512, 5], [16, 2]], 0, 0)
 
-    def fill(s, c):
-        act(s, A("ones", 0, len(range(s[1], s[2], s[3]))), Fn.Copy, scale=c)
-
+    memset(A("ones", 512, 1024), 1.0)
     fill(A("zt", 0, 1024), 0.0)
     fill(A("zt", 1024, 1280), 0.0)
-
-    copy(A("lu", 0, 64), A("lui", 0, 64))
-    memset(A("cc1", 0, 1024), 0.0)
-    for a in range(4):
-        for e in range(4):
-            m = 32 * a + 16 * (e // 2)
-            s = A("cc1", 4 * m + e, 4 * (m + 16), 4)
-            emit("v", lambda: g.vector.memset(T.cc1[32 * a:32 * a + 32, s[1]:s[2]:4], 1.0), [s], [], loose=True)
     ts(pcol(1), pcol(0), 15, None, Op.bitwise_and)
     ts(pcol(2), pcol(0), 31, None, Op.bitwise_and)
     ts(pcol(3), pcol(0), 4, None, Op.arith_shift_right)
-    ts(A("cc1", 512, 1024), A("cc1", 0, 512), 0.5, None, Op.mult)
-    quant("k1", 0, 256, "cc1", 0)
+    memset(A("cc1", 0, 512), 0.0)
+    for a in range(4):
+        for gg in range(2):
+            m = 32 * a + 16 * gg
+            s = A("cc1", 4 * m + gg, 4 * (m + 16), 2)
+            emit("v", lambda: g.vector.memset(T.cc1[32 * a:32 * a + 32, s[1]:s[2]:2], 1.0), [s], [], loose=True)
     copy(A("sc", 0, 3), A("pi", 1, 4))
+    memset(A("two", 0, 8), 2.0)
+    ts(A("cc1", 512, 1024), A("cc1", 0, 512), 0.5, None, Op.mult)
+    copy(A("lu", 0, 24), A("lui", 0, 24))
     quant("uq", 0, 128, "ut", 0)
     lst = A("lu", 0, 24)
     emit("a", lambda: g.scalar.activation(T.uss[:, 0:384], T.uqs[:, 0:128].indirect(ap(lst)), Fn.Copy), [A("uss", 0, 384)], [A("uqs", 0, 128), lst])
     emit("v", lambda: g.vector.tensor_copy(T.us[:, 0:384].bitcast(dt.uint32), T.uq[:, 0:128].bitcast(dt.uint32).indirect(ap(lst))),
          [A("us", 0, 384)], [A("uq", 0, 128), lst])
-    fill(A("ct5", 0, 1024), 0.0)
-    fill(A("ct5", 1024, 1280), 0.0)
-    ts(col(3), col(0), 8.0, col(2), Op.mult, Op.add)
-    ts(col(4), col(3), -1.0, -0.5, Op.mult, Op.add)
-    ts(col(5), col(3), -1.0, None, Op.mult)
-    ts(col(18), col(0), -1.0, None, Op.mult)
+
+    def consts_early():
+        copy(A("lu", 24, 64), A("lui", 24, 64))
+        quant("k1", 0, 256, "cc1", 0)
 
     def consts_a():
-        act(A("sgn", 0, 512), A("om", 0, 512), Fn.Sign, bias=col(4))
-        act(A("cst", 0, 512), A("sgn", 0, 512), Fn.Relu, scale=2.0)
-        act(A("cst", 512, 1024), A("sgn", 0, 512), Fn.Relu, scale=-2.0)
-        act(A("sg2", 0, 512), A("om", 0, 512), Fn.Abs, bias=col(5))
-        act(A("cst", 1024, 1536), A("sg2", 0, 512), Fn.Relu, bias=2.0, scale=-2.0)
-        fill(A("cst", 1536, 2048), 2.0)
         fill(A("cst", 2048, 3072), 0.0)
         fill(A("cst", 3072, 4096), 0.0)
         for b in range(4):
             for e in range(b + 1):
                 s = A("cst", 2048 + 512 * b + 4 * (3 + e // 2) + e, 2048 + 512 * b + 512, 64)
                 if e < b:
-                    fill(s, 2.0)
+                    iota(s, [[0, 8]], 2, 0)
                 else:
-                    act(s, A("gm", 0, 8), Fn.Copy)
+                    select(s, A("two", 0, 8), [[16, 8]], Op.is_gt, 0, -1)
+        fill(A("ct5", 0, 1024), 0.0)
+        fill(A("ct5", 1024, 1280), 0.0)
+
+    def consts_a2():
+        fill(A("fs", 0, 528), 0.0)
+        fill(A("cst", 1536, 2048), 2.0)
         fill(A("cci", 0, 640), 0.0)
         for e, c in ((80, -1.0), (86, -1.0), (121, 1.0), (127, 1.0)):
             fill(A("cci", e, e + 1), c)
-        act(A("eqt", 0, 320), A("jj", 0, 320), Fn.Abs, bias=col(18))
-        act(A("m16", 0, 320), A("eqt", 0, 320), Fn.Relu, bias=1.0, scale=-1.0)
         act(A("smk", 0, 80), A("smk", 0, 80), Fn.Sign)
         fill(A("z80", 0, 80), 0.0)
         fill(A("st", 0, 8), 0.0)
         fill(A("vf", 0, 32), 0.0)
-        fill(A("fs", 0, 528), 0.0)
 
     def consts_v():
+        ts(col(3), col(0), 8.0, col(2), Op.mult, Op.add)
         none, big, small = 1.5 * 2.0 ** 35, 1.5 * 2.0 ** 30, 1.5 * 2.0 ** 26
         ts(col(8), col(0), 3.0, none, Op.is_ge, Op.mult)
         for k, v in ((9, big), (10, small)):
@@ -288,16 +279,20 @@ def rank_program(g, core, T, topo):
         for k, v in ((11, none), (12, big), (13, small)):
             ts(col(k), col(0), float(k - 11), v, Op.is_equal, Op.mult)
         ts(col(14), col(2), 2.0, None, Op.mult)
+        ts(A("cst", 0, 512), A("om", 0, 512), col(3), 2.0, Op.is_gt, Op.mult)
         tt(col(19), col(8), col(9), Op.add)
         tt(col(20), col(8), col(11), Op.add)
         tt(col(21), col(12), col(13), Op.add)
+        ts(A("cst", 512, 1024), A("om", 0, 512), col(3), 2.0, Op.is_le, Op.mult)
         ts(col(15), col(0), 32.0, col(14), Op.mult, Op.add)
         ts(col(16), col(2), -1.0, 8.0, Op.mult, Op.add)
         tt(col(6), col(19), col(10), Op.add)
         tt(col(7), col(20), col(21), Op.add)
+        ts(A("cst", 1024, 1536), A("om", 0, 512), col(3), 2.0, Op.is_equal, Op.mult)
         ts(A("s2", 0, 20), A("s2", 0, 20), col(15), None, Op.add)
         ts(col(17), col(2), -2.0, 16.0, Op.mult, Op.add)
         ts(A("pl", 0, 20), A("pl", 0, 20), col(3), 0.5, Op.add, Op.add)
+        ts(A("m16", 0, 320), A("jj", 0, 320), col(0), None, Op.is_equal)
         ts(A("sz", 0, 20), A("s2", 0, 20), col(16), None, Op.add)
         quant("kc", 0, 512, "cst", 0)
         quant("kc", 512, 512, "cst", 2048)
@@ -307,15 +302,20 @@ def rank_program(g, core, T, topo):
 
     def other():
         flip[0] += 1
-        return "va"[flip[0] % 2]
+        return "vavav"[flip[0] % 5]
 
     def unpack(pair, b, d, bank, q, i):
         mm(bank, "er", 256 * b + 16 * d, pair, 0, H)
-        o = A("wv", 2560 * b + 2 * d + i, 2560 * b + 2560, 16)
+        k = 5120 * i + 640 * d + 160 * b
         if q == "v":
-            copy(o, P(bank, H))
+            copy(A("wv", k, k + H), P(bank, H))
         else:
-            act(o, P(bank, H), Fn.Copy)
+            act(A("wv", k, k + H), P(bank, H), Fn.Copy)
+
+    def by_dma(name, w, d):
+        o, i, k = A(name, w * d, w * d + w), A(name, 0, w), 128 - 16 * d
+        dma("s", T[name][0:k, o[1]:o[2]], T[name][16 * d:128, 0:w], [o], [i], loose=True)
+        dma("s", T[name][k:128, o[1]:o[2]], T[name][0:16 * d, 0:w], [o], [i], loose=True)
 
     def layer(pair, tile, out):
         for b in range(4):
@@ -331,89 +331,109 @@ def rank_program(g, core, T, topo):
     def L(k):
         return A("li", 20 * k, 20 * k + 20)
 
+    def LF(k):
+        return A("lf", 20 * k, 20 * k + 20)
+
     def TW(b):
         return A("wt", 320 * b, 320 * b + 9280)
+
+    def WV(b):
+        return A("wv", 160 * b, 160 * b + 9760)
+
+    def own(gg, b):
+        return A("tr", 32 * b + 16 * gg, 32 * b + 16 * gg + 1)
+
+    def t_number(b, d):
+        bank = 6 + b % 2
+        if d == 0:
+            mm(bank, "e0", 128 * b, "xq", 0, C)
+        else:
+            mm(bank, "er", 256 * b + 16 * d, "xq", 0, C)
+        act(A("wt", 1280 * d + 320 * b, 1280 * d + 320 * b + 320), P(bank, C), Fn.Copy)
+
+    def compare(b):
+        for gg in range(2):
+            t, e, lo = "ct%d" % (b // 2), 2 * (b % 2) + gg, 32 * b + 32
+            ts(A(t, e, 4 * lo, 4), P(1 + gg, lo), own(gg, b), None, Op.is_lt)
+            if lo < C:
+                ts(A(t, 4 * lo + e, 1280, 4), P(1 + gg, C, lo), own(gg, b), None, Op.is_le)
+
+    def compare_a(b):
+        for gg in range(2):
+            t, e, lo, z = "ct%d" % (b // 2), 2 * (b % 2) + gg, 32 * b + 32, 320 * ((2 * b + gg) % 4)
+            act(A("zs", z, z + C), P(4 + gg, C), Fn.Sign, bias=own(gg, b), scale=-1.0)
+            act(A(t, e, 4 * lo, 4), A("zs", z, z + lo), Fn.Sign, bias=-0.5)
+            if lo < C:
+                act(A(t, 4 * lo + e, 1280, 4), A("zs", z + lo, z + C), Fn.Sign, bias=0.5)
+
+    def add_ranks(t, w, start, stop):
+        quant("cq%d" % t, 0, C, "ct%d" % t, 0)
+        mm(3, "k1", 128 * w, "cq%d" % t, 0, C, start=start, stop=stop)
+
+    def tie_rows():
+        for k in range(2):
+            gather("a", A("ob", 320 * k, 320 * k + 320), A("tr", 0, 320), A("lu", 24 + 20 * k, 44 + 20 * k))
 
     for rd in range(ROUNDS):
         dst = T.cores[rank ^ MASK[rd]]
         dma("s", T.wn[:, 0:1280], T.zt[:, :], [A("wn", 0, 1280)], [A("zt", 0, 1280)])
         dma("s", T.wn[:, 1280:2560], T.zt[:, :], [A("wn", 1280, 2560)], [A("zt", 0, 1280)])
         quant("xq", 0, C, "xin" if rd == 0 else "xn", 0)
-        for bank, k in ((0, 0), (1, 1), (2, 2), (4, 1), (5, 2)):
+        for bank, k in ((0, 0), (1, 1), (2, 2)):
             mm(bank, "us", 128 * k, "xq", 0, C)
         emit("v", lambda: g.vector.transpose(T.tr[:, 0:320], T.ps0[:, 0:320]), [A("tr", 0, 320)], [P(0, 320)])
-
-        def own(gg, b):
-            return A("tr", 32 * b + 16 * gg, 32 * b + 16 * gg + 1)
-
-        def t_number(b, d):
-            bank = 6 + b % 2
-            mm(bank, "er", 256 * b + 16 * d, "xq", 0, C)
-            act(A("wt", 1280 * d + 320 * b, 1280 * d + 320 * b + 320), P(bank, C), Fn.Copy)
-
-        def turns_by_dma():
-            for d in range(BY_PRODUCT, 8):
-                o, i, k = A("wt", 1280 * d, 1280 * d + 1280), A("wt", 0, 1280), 128 - 16 * d
-                dma("s", T.wt[0:k, o[1]:o[2]], T.wt[16 * d:128, 0:1280], [o], [i], loose=True)
-                dma("s", T.wt[k:128, o[1]:o[2]], T.wt[0:16 * d, 0:1280], [o], [i], loose=True)
-
-        def passes(t):
-            for gg, b in ((0, 2 * t), (0, 2 * t + 1), (1, 2 * t), (1, 2 * t + 1)):
-                e, lo = 2 * gg + b % 2, 32 * b + 32
-                ts(A("ct%d" % t, e, 4 * lo, 4), P(1 + gg, lo), own(gg, b), None, Op.is_lt)
-                if lo < C:
-                    ts(A("ct%d" % t, 4 * lo + e, 1280, 4), P(1 + gg, C, lo), own(gg, b), None, Op.is_le)
-
-        def passes_a(t):
-            for k, (gg, b) in enumerate(((0, 2 * t), (0, 2 * t + 1), (1, 2 * t), (1, 2 * t + 1))):
-                e, lo, z = 2 * gg + b % 2, 32 * b + 32, 320 * k
-                act(A("zs", z, z + C), P(4 + gg, C), Fn.Sign, bias=own(gg, b), scale=-1.0)
-                act(A("ct%d" % t, e, 4 * lo, 4), A("zs", z, z + lo), Fn.Sign, bias=-0.5)
-                if lo < C:
-                    act(A("ct%d" % t, 4 * lo + e, 1280, 4), A("zs", z + lo, z + C), Fn.Sign, bias=0.5)
-
-        def add_ranks(t, w, start, stop):
-            quant("cq%d" % t, 0, C, "ct%d" % t, 0)
-            mm(3, "k1", w, "cq%d" % t, 0, C, start=start, stop=stop)
-
-        for k in range(2):
-            gather("a", A("ob", 320 * k, 320 * k + 320), A("tr", 0, 320), A("lu", 24 + 20 * k, 44 + 20 * k))
         if rd == 0:
-            turn(0)
-            passes(0)
-            for b in range(1, 4):
-                turn(b)
-            ts(A("gm", 0, 8), A("gi", 0, 8), col(2), 2.0, Op.is_gt, Op.mult)
+            mm(4, "us", 128, "xq", 0, C)
+            mm(5, "us", 256, "xq", 0, C)
+            consts_early()
+            compare(0)
+            consts_a()
+            tie_rows()
+            compare(1)
+            add_ranks(0, 0, True, False)
+            quant("e0", 0, 512, "est", 0)
+            for b in range(4):
+                for k in range(2):
+                    to = 256 * b + 128 * k
+                    dma("s", T.er[:, to:to + 128].bitcast(dt.uint8), T.e0[:, 128 * b:128 * b + 128].bitcast(dt.uint8), [A("er", to, to + 128)], [A("e0", 128 * b, 128 * b + 128)])
+                    dma("s", T.ers[:, to:to + 128], T.e0s[:, 128 * b:128 * b + 128], [A("ers", to, to + 128)], [A("e0s", 128 * b, 128 * b + 128)])
         for b in range(4):
             t_number(b, 0)
-        turns_by_dma()
-        passes_a(4)
+        for d in range(T_PRODUCTS, 8):
+            by_dma("wt", 1280, d)
+        if rd > 0:
+            mm(4, "us", 128, "xq", 0, C)
+            mm(5, "us", 256, "xq", 0, C)
+            tie_rows()
+            compare(0)
+            compare(1)
+            add_ranks(0, 0, True, False)
+        for b in BY_SCALAR:
+            compare_a(b)
         if rd == 0:
-            consts_a()
-        else:
-            passes(0)
-        add_ranks(0, 0, True, False)
-        passes(1)
+            consts_a2()
+        compare(2)
+        compare(3)
         add_ranks(1, 0, False, False)
-        for b in range(4):
-            t_number(b, 1)
+        compare(4)
+        compare(5)
+        add_ranks(2, 0, False, False)
         if rd == 0:
             ts(A("m32", 0, 320), A("jj", 320, 640), col(1), None, Op.is_gt)
-        passes(2)
-        add_ranks(2, 0, False, False)
         for gg in range(2):
             o = A("eqt", 320 * gg, 320 * gg + 320)
             tt(o, P(1 + gg, C), A("ob", 320 * gg, 320 * gg + 320), Op.is_equal)
-            tt(A("ct5", 2 * gg, 1280, 4), o, A("m32", 0, 320), Op.mult)
+            tt(A("ct5", gg, 1280, 4), o, A("m32", 0, 320), Op.mult)
         add_ranks(5, 0, False, False)
-        add_ranks(4, 128, False, False)
         for b in range(4):
-            t_number(b, 2)
-        passes(3)
-        add_ranks(3, 0, False, True)
+            t_number(b, 1)
+        compare(6)
+        compare(7)
+        add_ranks(4, 1, False, False)
         if rd == 0:
             consts_v()
-        ts(A("hb", 0, 320), P(3, C), 128.0, 0.5, Op.is_lt, Op.subtract)
+        add_ranks(3, 0, False, True)
+        ts(A("hb", 0, 320), P(3, C), 160.0 - 16 * len(BY_SCALAR), 0.5, Op.is_lt, Op.subtract)
         tt(A("fs", 16, 336), A("hb", 0, 320), A("m16", 0, 320), Op.mult)
         quant("fq", 0, 132, "fs", 0)
         mm(0, "kc", 0, "fq", 4, 128, True, False)
@@ -425,8 +445,9 @@ def rank_program(g, core, T, topo):
         mm(3, "kc", 768, "fq", 4, 128)
         scan(A("su", 0, 80), P(0, 80), A("z80", 0, 80), -0.5, Op.add, Op.add)
         mm(0, "kc", 896, "fq", 4, 128)
-        for b in range(4):
-            t_number(b, 3)
+        for d in range(2, T_PRODUCTS):
+            for b in range(4):
+                t_number(b, d)
         scan(A("sg", 0, 80), A("smk", 0, 80), P(1, 80), 0.0, Op.mult, Op.add)
         scan(A("st", 8, 88), P(2, 80), A("z80", 0, 80), 0.0, Op.add, Op.add)
         n2, y, h2 = L(0), L(1), L(2)
@@ -456,9 +477,9 @@ def rank_program(g, core, T, topo):
         tt(L(8), P(1, 20), A("s2", 0, 20), Op.add)
         ts(L(9), L(7), 7, None, Op.bitwise_and)
         ts(L(10), L(8), 3, None, Op.arith_shift_right)
-        ts(L(21), L(9), 1280, None, Op.mult)
-        tt(L(11), L(21), L(10), Op.add)
-        copy(A("off", 0, 20), L(11))
+        ts(L(11), L(9), 1280, None, Op.mult)
+        tt(L(12), L(11), L(10), Op.add)
+        copy(A("off", 0, 20), L(12))
         for b in range(4):
             gather("va"[b % 2], A("gt", b, 640, 4), TW(b), A("off", 10, 20))
         quant("gq", 0, H, "gt", 0)
@@ -467,23 +488,28 @@ def rank_program(g, core, T, topo):
             gather("va"[b % 2], A("ft", b, 640, 4), TW(b), A("off", 0, 10))
         quant("fqq", 0, H, "ft", 0)
         layer("fqq", "at", "aq")
-        turns = [(b, d) for b in range(4) for d in range(8)]
-        for k, (b, d) in enumerate(turns[:8]):
-            unpack("aq", b, d, 4 + k % 4, other(), 0)
+        for b in range(4):
+            unpack("aq", b, 0, 4 + b, "va"[b % 2], 0)
+        for d in range(A_PRODUCTS, 8):
+            by_dma("wv", 640, d)
         layer("gl%d" % rd, "bt", "bq")
         send(dst, "bq", "bl%d" % rd, "ba%d" % rd, "bs%d" % rd)
-        for k, (b, d) in enumerate(turns[8:]):
-            unpack("aq", b, d, 4 + k % 4, other(), 0)
-        ts(L(12), n2, 16, None, Op.bitwise_and)
-        ts(L(13), y, -8, None, Op.mult)
-        ts(L(14), n2, col(17), None, Op.add)
-        ts(L(15), L(12), 15.5, None, Op.mult)
-        tt(L(16), n2, L(13), Op.add)
-        ts(L(17), L(14), 14, None, Op.bitwise_and)
-        tt(L(18), L(16), L(15), Op.add)
-        tt(L(19), L(17), h2, Op.subtract)
-        tt(L(20), L(18), L(19), Op.add)
-        copy(A("wl", 0, 20), L(20))
+        for k in range(4 * (A_PRODUCTS - 1)):
+            unpack("aq", k % 4, 1 + k // 4, 4 + k % 4, other(), 0)
+        ts(L(13), n2, 4, None, Op.arith_shift_right)
+        ts(L(14), n2, 16, None, Op.bitwise_and)
+        ts(L(15), n2, 1, None, Op.bitwise_and)
+        ts(L(16), n2, col(17), None, Op.add)
+        ts(LF(0), y, -0.5, None, Op.mult)
+        ts(LF(1), L(14), 0.96875, None, Op.mult)
+        ts(LF(2), L(15), 5120.0, None, Op.mult)
+        ts(L(17), L(16), 14, None, Op.bitwise_and)
+        tt(LF(3), LF(0), L(13), Op.add)
+        tt(LF(4), LF(1), LF(2), Op.add)
+        ts(LF(5), L(17), 320.0, None, Op.mult)
+        tt(LF(6), LF(3), LF(4), Op.add)
+        tt(LF(7), LF(6), LF(5), Op.add)
+        copy(A("wl", 0, 20), LF(7))
         if rd == 0:
             quant("vq", 0, 128, "vt", 0)
         if rd == ROUNDS - 1:
@@ -498,12 +524,12 @@ def rank_program(g, core, T, topo):
                 dma("s", T.op[k:k + 1, :], T.vtr[32 * a:32 * a + 20, o:o + 16], [], [A("vtr", 0, 32)])
 
         def add_gathered(b, a, n):
-            o, win, t2 = A("xn", 4 * a + b, 4 * (a + n), 4), A("wv", 2560 * b, 2560 * b + 2560), A("wt", 320 * b + a, 320 * b + a + n)
+            o, win, t2 = A("xn", 4 * a + b, 4 * (a + n), 4), WV(b), A("wt", 320 * b + a, 320 * b + a + n)
             li = A("wl", a // 16, (a + n) // 16)
             emit("v", lambda: g.vector.tensor_tensor(ap(o), ap(win).indirect(ap(li)), ap(t2), Op.add), [o], [win, li, t2])
 
         def gather_v(b, slot, a, n):
-            gather("a", A("vb", 320 * slot + a, 320 * slot + a + n), A("wv", 2560 * b, 2560 * b + 2560), A("wl", a // 16, (a + n) // 16))
+            gather("a", A("vb", 320 * slot + a, 320 * slot + a + n), WV(b), A("wl", a // 16, (a + n) // 16))
 
         def add_v(b, slot, a, n):
             tt(A("xn", 4 * a + b, 4 * (a + n), 4), A("vb", 320 * slot + a, 320 * slot + a + n), A("wt", 320 * b + a, 320 * b + a + n), Op.add)
@@ -512,10 +538,8 @@ def rank_program(g, core, T, topo):
         for b in range(4):
             for d in range(8):
                 unpack(land, b, d, d, other(), 1)
-            if b == 1:
-                add_gathered(0, 0, 320)
-            if b == 2:
-                gather_v(1, 0, 0, 320)
+        gather_v(1, 0, 0, 320)
+        add_gathered(0, 0, 320)
         gather_v(2, 1, 0, 320)
         add_v(1, 0, 0, 320)
         add_gathered(3, 0, 160)

import math
from concourse.mybir import dt, AluOpType as Op, ActivationFunctionType as Fn

C, H, ROUNDS = 320, 160, 3
MASK = [1, 2, 3]
U8, F8, BF, F32, I32, U16 = "uint8", "float8_e4m3fn_x4", "bfloat16", "float32", "int32", "uint16"
T_PRODUCTS, A_PRODUCTS = 4, 4
BY_SCALAR = [8, 9]

SCRATCH = {}


def _sb(name, cols, dtype):
    SCRATCH[name] = ("sbuf", [128, cols], dtype)


def _mx(name, cols):
    _sb(name, cols, F8)
    _sb(name + "s", cols, U8)


for _k in range(8):
    SCRATCH["ps%d" % _k] = ("psum", [128, 512], F32)
for _n, _w in (("xin", 1280), ("xn", 1280), ("ut", 512), ("vt", 512), ("ones", 1024), ("zt", 1280), ("hb", 320), ("eqt", 640), ("zs", 1280),
               ("fs", 528), ("dat", 320), ("wn", 2560), ("wt", 10240), ("wv", 10240), ("gt", 640), ("ft", 640), ("at", 640),
               ("bt", 640), ("vb", 640), ("m16", 320), ("m32", 320), ("est", 2048), ("cst", 4096), ("cc1", 1024), ("cci", 640), ("two", 8)):
    _sb(_n, _w, BF)
for _k in range(6):
    _sb("ct%d" % _k, 1280, BF)
    _mx("cq%d" % _k, 320)
for _n, _w in (("tr", 320), ("ob", 640), ("su", 80), ("sg", 80), ("st", 96), ("r1", 80), ("r0", 80), ("dg", 80), ("n2f", 32),
               ("vf", 32), ("vtr", 32), ("om", 512), ("jj", 640), ("sc", 32), ("pl", 20), ("s2", 20), ("sz", 20), ("it", 20),
               ("smk", 80), ("z80", 80), ("yo", 320), ("lf", 200)):
    _sb(_n, _w, F32)
for _n, _w in (("pi", 8), ("lui", 64), ("li", 480)):
    _sb(_n, _w, I32)
for _n, _w in (("lu", 64), ("pos", 32), ("off", 32), ("wl", 32)):
    _sb(_n, _w, U16)
for _n, _w in (("xq", 320), ("uq", 128), ("us", 384), ("vq", 128), ("wq", 512), ("e0", 512), ("er", 1024), ("kc", 1024), ("k1", 256),
               ("ki", 160), ("fq", 132), ("nq", 640), ("gq", 160), ("fqq", 160), ("aq", 160), ("bq", 160)):
    _mx(_n, _w)
for _k in range(ROUNDS):
    _mx("gl%d" % _k, 160)
    _mx("bl%d" % _k, 160)

SEMAPHORES = ["ev", "ea", "et", "ep"] + ["d%d" % _k for _k in range(120)]
for _k in range(ROUNDS):
    SEMAPHORES += ["ga%d" % _k, "ba%d" % _k, "gs%d" % _k, "bs%d" % _k]


def rank_program(g, core, T, topo):
    rank = T.rank_of(core)
    if rank is None:
        return
    queue = {"v": g.vector, "a": g.scalar, "t": g.tensor, "p": g, "s": g.sync}
    known = {q: {} for q in queue}
    count, snaps, log, ndma, final = {}, {}, {}, [0], {}

    def A(name, a, b, step=1):
        return (name, a, b, step)

    def ap(s):
        return T[s[0]][:, s[1]:s[2]] if s[3] == 1 else T[s[0]][:, s[1]:s[2]:s[3]]

    def hit(x, y):
        return x[1] < y[2] and y[1] < x[2] and (x[1] - y[1]) % math.gcd(x[3], y[3]) == 0

    def need(q, tokens):
        for tok in sorted(set(tokens), key=lambda k: (k[0], -k[1])):
            if known[q].get(tok[0], 0) < tok[1]:
                queue[q].wait_ge(T.sem[tok[0]], tok[1])
                known[q][tok[0]] = tok[1]
                for s, n in snaps[tok].items():
                    known[q][s] = max(known[q].get(s, 0), n)

    def note(s, w, q, token, loose=False):
        keep = []
        for r in log.get(s[0], []):
            x = r[0]
            inside = s[1] <= x[1] and x[2] <= s[2] and (s[3] == 1 or (s[3] == x[3] and (s[1] - x[1]) % s[3] == 0))
            if loose or not (inside and (w or (r[2] == q and not r[1]))):
                keep.append(r)
        keep.append((s, w, q, token, loose))
        log[s[0]] = keep

    def emit(q, fn, outs, ins, token=None, acc=False, loose=False):
        tokens = []
        for lst, w in ((ins, False), (outs, True)):
            for s in lst:
                bank = s[0][:2] == "ps"
                for r in log.get(s[0], ()):
                    if bank:
                        if not (r[2] == q and (acc or not (w or r[1]))):
                            tokens.append(r[3])
                    elif loose and w and r[1] and r[2] == q and r[4]:
                        continue
                    elif (w or r[1]) and hit(s, r[0]):
                        tokens.append(r[3])
        need(q, tokens)
        inst = fn()
        if token is None:
            name = "e" + q
            count[name] = count.get(name, 0) + 1
            token = (name, count[name])
            inst.then_inc(T.sem[name], 1)
        final[token[0]] = token[1]
        snaps[token] = dict(known[q])
        for s in ins:
            note(s, False, q, token, q == "s")
        for s in outs:
            note(s, True, q, token, loose)

    def dma(q, out_ap, in_ap, outs, ins, loose=False):
        tok = ("d%d" % ndma[0], 16)
        ndma[0] += 1
        emit(q, lambda: queue[q].dma_start(out_ap, in_ap).then_inc(T.sem[tok[0]], 16), outs, ins, tok, loose=loose)

    def memset(s, c):
        emit("v", lambda: g.vector.memset(ap(s), c), [s], [])

    def copy(o, i):
        emit("v", lambda: g.vector.tensor_copy(ap(o), ap(i)), [o], [i])

    def tt(o, a, b, op):
        emit("v", lambda: g.vector.tensor_tensor(ap(o), ap(a), ap(b), op), [o], [a, b])

    def ts(o, a, c1, c2, op0, op1=None):
        ins = [a] + [c for c in (c1, c2) if isinstance(c, tuple)]
        x1 = ap(c1) if isinstance(c1, tuple) else c1
        x2 = ap(c2) if isinstance(c2, tuple) else c2
        if op1 is None:
            emit("v", lambda: g.vector.tensor_scalar(ap(o), ap(a), x1, None, op0), [o], ins)
        else:
            emit("v", lambda: g.vector.tensor_scalar(ap(o), ap(a), x1, x2, op0, op1), [o], ins)

    def scan(o, a, b, init, op0, op1):
        emit("v", lambda: g.vector.tensor_tensor_scan(ap(o), ap(a), ap(b), init, op0, op1), [o], [a, b])

    def act(o, i, fn, bias=None, scale=1.0):
        if bias is None:
            emit("a", lambda: g.scalar.activation(ap(o), ap(i), fn, scale=scale), [o], [i])
        elif isinstance(bias, tuple):
            emit("a", lambda: g.scalar.activation(ap(o), ap(i), fn, bias=ap(bias), scale=scale), [o], [i, bias])
        else:
            emit("a", lambda: g.scalar.activation(ap(o), ap(i), fn, bias=bias, scale=scale), [o], [i])

    def quant(o, c, n, i, c2):
        src = A(i, c2, c2 + 4 * n)
        emit("v", lambda: g.vector.quantize_mx(T[o][:, c:c + n], T[o + "s"][:, c:c + n], ap(src)), [A(o, c, c + n), A(o + "s", c, c + n)], [src])

    def mm(bank, w, wc, x, xc, n, start=True, stop=True):
        o = A("ps%d" % bank, 0, 512)
        emit("t", lambda: g.tensor.matmul_mx(T["ps%d" % bank][:, 0:n], T[w][:, wc:wc + 128], T[w + "s"][:, wc:wc + 128],
                                             T[x][:, xc:xc + n], T[x + "s"][:, xc:xc + n], start, stop),
             [o], [A(w, wc, wc + 128), A(w + "s", wc, wc + 128), A(x, xc, xc + n), A(x + "s", xc, xc + n)], acc=not start)

    def P(bank, n, a=0):
        return A("ps%d" % bank, a, n)

    def gather(q, o, win, lst):
        if q == "v":
            emit("v", lambda: g.vector.tensor_copy(ap(o), ap(win).indirect(ap(lst))), [o], [win, lst])
        else:
            emit("a", lambda: g.scalar.activation(ap(o), ap(win).indirect(ap(lst)), Fn.Copy), [o], [win, lst])

    def send(dst, src, land, sem, done):
        rid, pid, _ = topo.addr(dst)
        eng = topo.engines(core, dst)
        ec, es = eng[0::2], eng[1::4]
        total = len(ec) + len(es)
        need("p", [r[3] for nm in (src, src + "s") for r in log[nm] if r[1]])
        g.remote_dma(T[land][:, 0:H].bitcast(dt.uint8), T[src][:, 0:H].bitcast(dt.uint8), T.sem[sem], T.sem[done], pid, rid, sum(1 << e for e in ec))
        g.remote_dma(T[land + "s"][:, 0:H], T[src + "s"][:, 0:H], T.sem[sem], T.sem[done], pid, rid, sum(1 << e for e in es))
        tok, arr = (done, total), (sem, total)
        snaps[tok], snaps[arr] = dict(known["p"]), {}
        final[done], final[sem] = total, total
        for nm in (src, src + "s"):
            note(A(nm, 0, H), False, "p", tok)
        for nm in (land, land + "s"):
            log[nm] = [(A(nm, 0, H), True, "r", arr, False)]

    def iota(o, pattern, base, cm):
        if o[0] in ("pi", "lui"):
            emit("p", lambda: g.iota(ap(o), pattern, base, cm), [o], [])
        else:
            emit("p", lambda: g.iota(ap(o), pattern, base, cm, allow_small_or_imprecise_dtypes=True), [o], [])

    def select(o, i, pattern, cmp, base, cm):
        emit("p", lambda: g.affine_select(ap(o), ap(i), pattern, cmp, 0.0, base, cm), [o], [i])

    def pcol(k):
        return A("pi", k, k + 1)

    def col(k):
        return A("sc", k, k + 1)

    def fill(s, c):
        act(s, A("ones", 0, len(range(s[1], s[2], s[3]))), Fn.Copy, scale=c)

    dma("a", T.ut[:, :], T.u[:, :], [A("ut", 0, 512)], [])
    dma("s", T.xin[:, :], T.x[:, :], [A("xin", 0, 1280)], [])
    dma("s", T.wq[:, :].bitcast(dt.uint8), T.wc[:, :], [A("wq", 0, 512)], [])
    dma("s", T.wqs[:, :], T.ws[:, :], [A("wqs", 0, 512)], [])
    dma("s", T.vt[:, :], T.v[:, :], [A("vt", 0, 512)], [])

    memset(A("ones", 0, 512), 1.0)
    iota(A("pi", 0, 1), [[0, 1]], 0, 1)
    iota(A("lui", 0, 8), [[16, 8]], 0, 0)
    iota(A("lui", 8, 16), [[32, 4], [0, 2]], 0, 0)
    iota(A("lui", 16, 24), [[32, 4], [0, 2]], 16, 0)
    for b in range(4):
        select(A("est", 512 * b, 512 * b + 512), A("ones", 0, 512), [[-1, 128], [1000, 4]], Op.is_equal, -1000 * b, 1)
        if b == 0:
            iota(A("lui", 24, 44), [[32, 10], [0, 2]], 0, 0)
            iota(A("lui", 44, 64), [[32, 10], [0, 2]], 16, 0)
    iota(A("om", 0, 512), [[1, 8], [8, 16], [0, 4]], 0, 0)
    iota(A("jj", 320, 640), [[0, 10], [1, 32]], 0, 0)
    iota(A("jj", 0, 320), [[0, 20], [1, 16]], 0, 0)
    iota(A("smk", 0, 80), [[0, 20], [1, 4]], 0, 0)
    iota(A("pl", 0, 20), [[128, 20]], 0, 0)
    iota(A("s2", 0, 20), [[0, 2], [512, 5], [16, 2]], 0, 0)

    memset(A("ones", 512, 1024), 1.0)
    fill(A("zt", 0, 1024), 0.0)
    fill(A("zt", 1024, 1280), 0.0)
    ts(pcol(1), pcol(0), 15, None, Op.bitwise_and)
    ts(pcol(2), pcol(0), 31, None, Op.bitwise_and)
    ts(pcol(3), pcol(0), 4, None, Op.arith_shift_right)
    memset(A("cc1", 0, 512), 0.0)
    for a in range(4):
        for gg in range(2):
            m = 32 * a + 16 * gg
            s = A("cc1", 4 * m + gg, 4 * (m + 16), 2)
            emit("v", lambda: g.vector.memset(T.cc1[32 * a:32 * a + 32, s[1]:s[2]:2], 1.0), [s], [], loose=True)
    copy(A("sc", 0, 3), A("pi", 1, 4))
    memset(A("two", 0, 8), 2.0)
    ts(A("cc1", 512, 1024), A("cc1", 0, 512), 0.5, None, Op.mult)
    copy(A("lu", 0, 24), A("lui", 0, 24))
    quant("uq", 0, 128, "ut", 0)
    lst = A("lu", 0, 24)
    emit("a", lambda: g.scalar.activation(T.uss[:, 0:384], T.uqs[:, 0:128].indirect(ap(lst)), Fn.Copy), [A("uss", 0, 384)], [A("uqs", 0, 128), lst])
    emit("v", lambda: g.vector.tensor_copy(T.us[:, 0:384].bitcast(dt.uint32), T.uq[:, 0:128].bitcast(dt.uint32).indirect(ap(lst))),
         [A("us", 0, 384)], [A("uq", 0, 128), lst])

    def consts_early():
        copy(A("lu", 24, 64), A("lui", 24, 64))
        quant("k1", 0, 256, "cc1", 0)

    def consts_a():
        fill(A("cst", 2048, 3072), 0.0)
        fill(A("cst", 3072, 4096), 0.0)
        for b in range(4):
            for e in range(b + 1):
                s = A("cst", 2048 + 512 * b + 4 * (3 + e // 2) + e, 2048 + 512 * b + 512, 64)
                if e < b:
                    iota(s, [[0, 8]], 2, 0)
                else:
                    select(s, A("two", 0, 8), [[16, 8]], Op.is_gt, 0, -1)
        fill(A("ct5", 0, 1024), 0.0)
        fill(A("ct5", 1024, 1280), 0.0)

    def consts_a2():
        fill(A("fs", 0, 528), 0.0)
        fill(A("cst", 1536, 2048), 2.0)
        fill(A("cci", 0, 640), 0.0)
        for e, c in ((80, -1.0), (86, -1.0), (121, 1.0), (127, 1.0)):
            fill(A("cci", e, e + 1), c)
        act(A("smk", 0, 80), A("smk", 0, 80), Fn.Sign)
        fill(A("z80", 0, 80), 0.0)
        fill(A("st", 0, 8), 0.0)
        fill(A("vf", 0, 32), 0.0)

    def consts_v():
        ts(col(3), col(0), 8.0, col(2), Op.mult, Op.add)
        none, big, small = 1.5 * 2.0 ** 35, 1.5 * 2.0 ** 30, 1.5 * 2.0 ** 26
        ts(col(8), col(0), 3.0, none, Op.is_ge, Op.mult)
        for k, v in ((9, big), (10, small)):
            ts(col(k), col(0), float(k - 9), v, Op.is_equal, Op.mult)
        for k, v in ((11, none), (12, big), (13, small)):
            ts(col(k), col(0), float(k - 11), v, Op.is_equal, Op.mult)
        ts(col(14), col(2), 2.0, None, Op.mult)
        ts(A("cst", 0, 512), A("om", 0, 512), col(3), 2.0, Op.is_gt, Op.mult)
        tt(col(19), col(8), col(9), Op.add)
        tt(col(20), col(8), col(11), Op.add)
        tt(col(21), col(12), col(13), Op.add)
        ts(A("cst", 512, 1024), A("om", 0, 512), col(3), 2.0, Op.is_le, Op.mult)
        ts(col(15), col(0), 32.0, col(14), Op.mult, Op.add)
        ts(col(16), col(2), -1.0, 8.0, Op.mult, Op.add)
        tt(col(6), col(19), col(10), Op.add)
        tt(col(7), col(20), col(21), Op.add)
        ts(A("cst", 1024, 1536), A("om", 0, 512), col(3), 2.0, Op.is_equal, Op.mult)
        ts(A("s2", 0, 20), A("s2", 0, 20), col(15), None, Op.add)
        ts(col(17), col(2), -2.0, 16.0, Op.mult, Op.add)
        ts(A("pl", 0, 20), A("pl", 0, 20), col(3), 0.5, Op.add, Op.add)
        ts(A("m16", 0, 320), A("jj", 0, 320), col(0), None, Op.is_equal)
        ts(A("sz", 0, 20), A("s2", 0, 20), col(16), None, Op.add)
        quant("kc", 0, 512, "cst", 0)
        quant("kc", 512, 512, "cst", 2048)
        quant("ki", 0, 160, "cci", 0)

    flip = [0]

    def other():
        flip[0] += 1
        return "vavav"[flip[0] % 5]

    def unpack(pair, b, d, bank, q, i):
        mm(bank, "er", 256 * b + 16 * d, pair, 0, H)
        k = 5120 * i + 640 * d + 160 * b
        if q == "v":
            copy(A("wv", k, k + H), P(bank, H))
        else:
            act(A("wv", k, k + H), P(bank, H), Fn.Copy)

    def by_dma(name, w, d):
        o, i, k = A(name, w * d, w * d + w), A(name, 0, w), 128 - 16 * d
        dma("s", T[name][0:k, o[1]:o[2]], T[name][16 * d:128, 0:w], [o], [i], loose=True)
        dma("s", T[name][k:128, o[1]:o[2]], T[name][0:16 * d, 0:w], [o], [i], loose=True)

    def layer(pair, tile, out):
        for b in range(4):
            mm(b, "wq", 128 * b, pair, 0, H)
        for b in range(4):
            o = A(tile, b, 4 * H, 4)
            if b % 2 == 0:
                ts(o, P(b, H), 0.0, 0.03125, Op.max, Op.mult)
            else:
                act(o, P(b, H), Fn.Relu, scale=0.03125)
        quant(out, 0, H, tile, 0)

    def L(k):
        return A("li", 20 * k, 20 * k + 20)

    def LF(k):
        return A("lf", 20 * k, 20 * k + 20)

    def TW(b):
        return A("wt", 320 * b, 320 * b + 9280)

    def WV(b):
        return A("wv", 160 * b, 160 * b + 9760)

    def own(gg, b):
        return A("tr", 32 * b + 16 * gg, 32 * b + 16 * gg + 1)

    def t_number(b, d):
        bank = 6 + b % 2
        if d == 0:
            mm(bank, "e0", 128 * b, "xq", 0, C)
        else:
            mm(bank, "er", 256 * b + 16 * d, "xq", 0, C)
        act(A("wt", 1280 * d + 320 * b, 1280 * d + 320 * b + 320), P(bank, C), Fn.Copy)

    def compare(b):
        for gg in range(2):
            t, e, lo = "ct%d" % (b // 2), 2 * (b % 2) + gg, 32 * b + 32
            ts(A(t, e, 4 * lo, 4), P(1 + gg, lo), own(gg, b), None, Op.is_lt)
            if lo < C:
                ts(A(t, 4 * lo + e, 1280, 4), P(1 + gg, C, lo), own(gg, b), None, Op.is_le)

    def compare_a(b):
        for gg in range(2):
            t, e, lo, z = "ct%d" % (b // 2), 2 * (b % 2) + gg, 32 * b + 32, 320 * ((2 * b + gg) % 4)
            act(A("zs", z, z + C), P(4 + gg, C), Fn.Sign, bias=own(gg, b), scale=-1.0)
            act(A(t, e, 4 * lo, 4), A("zs", z, z + lo), Fn.Sign, bias=-0.5)
            if lo < C:
                act(A(t, 4 * lo + e, 1280, 4), A("zs", z + lo, z + C), Fn.Sign, bias=0.5)

    def add_ranks(t, w, start, stop):
        quant("cq%d" % t, 0, C, "ct%d" % t, 0)
        mm(3, "k1", 128 * w, "cq%d" % t, 0, C, start=start, stop=stop)

    def tie_rows():
        for k in range(2):
            gather("a", A("ob", 320 * k, 320 * k + 320), A("tr", 0, 320), A("lu", 24 + 20 * k, 44 + 20 * k))

    for rd in range(ROUNDS):
        dst = T.cores[rank ^ MASK[rd]]
        dma("s", T.wn[:, 0:1280], T.zt[:, :], [A("wn", 0, 1280)], [A("zt", 0, 1280)])
        dma("s", T.wn[:, 1280:2560], T.zt[:, :], [A("wn", 1280, 2560)], [A("zt", 0, 1280)])
        quant("xq", 0, C, "xin" if rd == 0 else "xn", 0)
        for bank, k in ((0, 0), (1, 1), (2, 2)):
            mm(bank, "us", 128 * k, "xq", 0, C)
        emit("v", lambda: g.vector.transpose(T.tr[:, 0:320], T.ps0[:, 0:320]), [A("tr", 0, 320)], [P(0, 320)])
        if rd == 0:
            mm(4, "us", 128, "xq", 0, C)
            mm(5, "us", 256, "xq", 0, C)
            consts_early()
            compare(0)
            consts_a()
            tie_rows()
            compare(1)
            add_ranks(0, 0, True, False)
            quant("e0", 0, 512, "est", 0)
            for b in range(4):
                for k in range(2):
                    to = 256 * b + 128 * k
                    dma("s", T.er[:, to:to + 128].bitcast(dt.uint8), T.e0[:, 128 * b:128 * b + 128].bitcast(dt.uint8), [A("er", to, to + 128)], [A("e0", 128 * b, 128 * b + 128)])
                    dma("s", T.ers[:, to:to + 128], T.e0s[:, 128 * b:128 * b + 128], [A("ers", to, to + 128)], [A("e0s", 128 * b, 128 * b + 128)])
        for b in range(4):
            t_number(b, 0)
        for d in range(T_PRODUCTS, 8):
            by_dma("wt", 1280, d)
        if rd > 0:
            mm(4, "us", 128, "xq", 0, C)
            mm(5, "us", 256, "xq", 0, C)
            tie_rows()
            compare(0)
            compare(1)
            add_ranks(0, 0, True, False)
        for b in BY_SCALAR:
            compare_a(b)
        if rd == 0:
            consts_a2()
        compare(2)
        compare(3)
        add_ranks(1, 0, False, False)
        compare(4)
        compare(5)
        add_ranks(2, 0, False, False)
        if rd == 0:
            ts(A("m32", 0, 320), A("jj", 320, 640), col(1), None, Op.is_gt)
        for gg in range(2):
            o = A("eqt", 320 * gg, 320 * gg + 320)
            tt(o, P(1 + gg, C), A("ob", 320 * gg, 320 * gg + 320), Op.is_equal)
            tt(A("ct5", gg, 1280, 4), o, A("m32", 0, 320), Op.mult)
        add_ranks(5, 0, False, False)
        for b in range(4):
            t_number(b, 1)
        compare(6)
        compare(7)
        add_ranks(4, 1, False, False)
        if rd == 0:
            consts_v()
        add_ranks(3, 0, False, True)
        ts(A("hb", 0, 320), P(3, C), 160.0 - 16 * len(BY_SCALAR), 0.5, Op.is_lt, Op.subtract)
        tt(A("fs", 16, 336), A("hb", 0, 320), A("m16", 0, 320), Op.mult)
        quant("fq", 0, 132, "fs", 0)
        mm(0, "kc", 0, "fq", 4, 128, True, False)
        mm(0, "kc", 128, "fq", 0, 128, False, True)
        mm(1, "kc", 256, "fq", 4, 128)
        mm(2, "kc", 384, "fq", 4, 128)
        mm(4, "kc", 512, "fq", 4, 128)
        mm(5, "kc", 640, "fq", 4, 128)
        mm(3, "kc", 768, "fq", 4, 128)
        scan(A("su", 0, 80), P(0, 80), A("z80", 0, 80), -0.5, Op.add, Op.add)
        mm(0, "kc", 896, "fq", 4, 128)
        for d in range(2, T_PRODUCTS):
            for b in range(4):
                t_number(b, d)
        scan(A("sg", 0, 80), A("smk", 0, 80), P(1, 80), 0.0, Op.mult, Op.add)
        scan(A("st", 8, 88), P(2, 80), A("z80", 0, 80), 0.0, Op.add, Op.add)
        n2, y, h2 = L(0), L(1), L(2)
        tt(A("n2f", 0, 20), A("su", 3, 80, 4), A("sg", 3, 80, 4), Op.mult)
        ts(A("r1", 0, 80), A("st", 7, 87), col(6), col(6), Op.add, Op.subtract)
        tt(n2, A("n2f", 0, 20), A("pl", 0, 20), Op.add)
        ts(A("r0", 0, 80), A("st", 7, 87), col(7), col(7), Op.add, Op.subtract)
        ts(y, n2, 4, 31, Op.arith_shift_right, Op.bitwise_and)
        ts(h2, n2, 14, None, Op.bitwise_and)
        tt(A("dg", 0, 80), A("r1", 0, 80), A("r0", 0, 80), Op.subtract)
        ts(L(3), y, -14, None, Op.mult)
        ts(L(4), h2, 31, None, Op.mult)
        for b, bank in ((0, 4), (1, 5)):
            tt(A("dat", b, 320, 4), P(bank, 80), A("dg", 0, 80), Op.add)
        tt(L(5), L(3), n2, Op.add)
        tt(A("dat", 2, 320, 4), P(3, 80), A("dg", 0, 80), Op.add)
        tt(L(6), L(5), L(4), Op.add)
        tt(A("dat", 3, 320, 4), P(0, 80), A("dg", 0, 80), Op.add)
        copy(A("pos", 0, 20), L(6))
        slots, lst = A("wn", 0, 2560), A("pos", 0, 20)
        emit("v", lambda: g.vector.tensor_copy(ap(slots).indirect(ap(lst)), T.dat[:, 0:320]), [slots], [lst, A("dat", 0, 320)])
        quant("nq", 0, 320, "wn", 0)
        quant("nq", 320, 320, "wn", 1280)
        for s in range(5):
            mm(1, "nq", 128 * s, "ki", 20 - 2 * s, 128, s == 0, s == 4)
        tt(L(7), P(1, 20), A("sz", 0, 20), Op.add)
        tt(L(8), P(1, 20), A("s2", 0, 20), Op.add)
        ts(L(9), L(7), 7, None, Op.bitwise_and)
        ts(L(10), L(8), 3, None, Op.arith_shift_right)
        ts(L(11), L(9), 1280, None, Op.mult)
        tt(L(12), L(11), L(10), Op.add)
        copy(A("off", 0, 20), L(12))
        for b in range(4):
            gather("va"[b % 2], A("gt", b, 640, 4), TW(b), A("off", 10, 20))
        quant("gq", 0, H, "gt", 0)
        send(dst, "gq", "gl%d" % rd, "ga%d" % rd, "gs%d" % rd)
        for b in range(4):
            gather("va"[b % 2], A("ft", b, 640, 4), TW(b), A("off", 0, 10))
        quant("fqq", 0, H, "ft", 0)
        layer("fqq", "at", "aq")
        for b in range(4):
            unpack("aq", b, 0, 4 + b, "va"[b % 2], 0)
        for d in range(A_PRODUCTS, 8):
            by_dma("wv", 640, d)
        layer("gl%d" % rd, "bt", "bq")
        send(dst, "bq", "bl%d" % rd, "ba%d" % rd, "bs%d" % rd)
        for k in range(4 * (A_PRODUCTS - 1)):
            unpack("aq", k % 4, 1 + k // 4, 4 + k % 4, other(), 0)
        ts(L(13), n2, 4, None, Op.arith_shift_right)
        ts(L(14), n2, 16, None, Op.bitwise_and)
        ts(L(15), n2, 1, None, Op.bitwise_and)
        ts(L(16), n2, col(17), None, Op.add)
        ts(LF(0), y, -0.5, None, Op.mult)
        ts(LF(1), L(14), 0.96875, None, Op.mult)
        ts(LF(2), L(15), 5120.0, None, Op.mult)
        ts(L(17), L(16), 14, None, Op.bitwise_and)
        tt(LF(3), LF(0), L(13), Op.add)
        tt(LF(4), LF(1), LF(2), Op.add)
        ts(LF(5), L(17), 320.0, None, Op.mult)
        tt(LF(6), LF(3), LF(4), Op.add)
        tt(LF(7), LF(6), LF(5), Op.add)
        copy(A("wl", 0, 20), LF(7))
        if rd == 0:
            quant("vq", 0, 128, "vt", 0)
        if rd == ROUNDS - 1:
            ts(A("r0", 0, 20), A("sg", 3, 80, 4), -639.75, None, Op.mult)
            ts(A("r1", 0, 20), A("n2f", 0, 20), 0.5, 639.75, Op.mult, Op.add)
            ts(A("it", 0, 20), A("pl", 0, 20), 0.5, None, Op.mult)
            tt(A("dg", 0, 20), A("r0", 0, 20), A("r1", 0, 20), Op.add)
            tt(A("vf", 0, 20), A("dg", 0, 20), A("it", 0, 20), Op.add)
            emit("v", lambda: g.vector.transpose(T.vtr[:, 0:32], T.vf[:, 0:32]), [A("vtr", 0, 32)], [A("vf", 0, 32)])
            for k in range(8):
                a, o = k // 2, 16 * (k % 2)
                dma("s", T.op[k:k + 1, :], T.vtr[32 * a:32 * a + 20, o:o + 16], [], [A("vtr", 0, 32)])

        def add_gathered(b, a, n):
            o, win, t2 = A("xn", 4 * a + b, 4 * (a + n), 4), WV(b), A("wt", 320 * b + a, 320 * b + a + n)
            li = A("wl", a // 16, (a + n) // 16)
            emit("v", lambda: g.vector.tensor_tensor(ap(o), ap(win).indirect(ap(li)), ap(t2), Op.add), [o], [win, li, t2])

        def gather_v(b, slot, a, n):
            gather("a", A("vb", 320 * slot + a, 320 * slot + a + n), WV(b), A("wl", a // 16, (a + n) // 16))

        def add_v(b, slot, a, n):
            tt(A("xn", 4 * a + b, 4 * (a + n), 4), A("vb", 320 * slot + a, 320 * slot + a + n), A("wt", 320 * b + a, 320 * b + a + n), Op.add)

        land = "bl%d" % rd
        for b in range(4):
            for d in range(8):
                unpack(land, b, d, d, other(), 1)
        gather_v(1, 0, 0, 320)
        add_gathered(0, 0, 320)
        gather_v(2, 1, 0, 320)
        add_v(1, 0, 0, 320)
        add_gathered(3, 0, 160)
        gather_v(3, 0, 160, 160)
        add_v(2, 1, 0, 320)
        add_v(3, 0, 160, 160)

    quant("xq", 0, C, "xn", 0)
    dma("s", T.oc[:, :], T.xq[:, 0:C].bitcast(dt.uint8), [], [A("xq", 0, C)])
    mm(0, "vq", 0, "xq", 0, C)
    for k in range(4):
        dma("a", T.osc[4 * k:4 * k + 4, :], T.xqs[32 * k:32 * k + 4, 0:C], [], [A("xqs", 0, C)])
    copy(A("yo", 0, C), P(0, C))
    dma("s", T.y[:, :], T.yo[:, 0:C], [], [A("yo", 0, C)])
    for s in sorted(final):
        if known["p"].get(s, 0) < final[s]:
            g.wait_ge(T.sem[s], final[s])
